import numpy as np, ml_dtypes
CORES = [83,85,87,115,117,119]
N = 6
BF = ml_dtypes.bfloat16
def gentries(a):
    return np.ascontiguousarray(a.reshape(8, 16, -1).transpose(0, 2, 1)).reshape(8, -1)
def gtable(e):
    e = np.asarray(e); return np.ascontiguousarray(e.reshape(8, -1, 16).transpose(0, 2, 1)).reshape(128, -1).astype(np.int32)
W, LW, M, K, CAP, RO = 2048, 11, 1536, 256, 96, 3
def h1(v):
    return ((v * v >> 3) + v) & (W - 1)
def h2(v):
    return ((v * v >> 5) + 37 * v + 1) & (W - 1)
def parts(rng):
    X = rng.integers(0, 16, (N, 8, 16, W)); F = rng.integers(0, W, (N, 8, 16, W)); LG = rng.integers(0, M, (N, 8, W))
    for q in range(N):
        for g in range(8):
            v = rng.permutation(M)[:7 * M // 10]
            LG[q, g, np.where(rng.random(len(v)) < 0.5, h1(v), h2(v))] = v
    LE = (rng.random((N, 8, W)) < rng.choice(np.array([0.3, 0.5, 0.7, 0.9]), (N, 8, 1))).astype(np.int64)
    XL = rng.integers(0, 16, (N, 8, 16, M)); LF = rng.integers(0, M, (N, 8, 16, M))
    return X, F, LG, LE, XL, LF, rng.integers(0, W, (N, 8, 16, K)), rng.integers(0, 16, (N, 8, 16, K))
def pack(X, F, LG, LE, XL, LF, C, Q):
    def bf(a): return np.ascontiguousarray(a).reshape(N, 128, -1).astype(np.float32).astype(BF)
    F = np.ascontiguousarray(F).reshape(N, 128, W)
    return {"xr": bf(X), "fd": (F[..., :W // 2] + W * F[..., W // 2:]).astype(np.int32), "tg": (2 * LG + LE).astype(np.int32), "xl": bf(XL),
            "lf": np.ascontiguousarray(LF).reshape(N, 128, M).astype(np.int32), "cx": np.stack([gtable(a.transpose(0, 2, 1).reshape(8, -1)) for a in C]), "qx": bf(Q)}
def setup_inputs(rng):
    return pack(*parts(rng))
def setup_inputs_spread(rng):
    X, F, LG, LE, XL, LF, C, Q = parts(rng)
    def small(n): return np.minimum((np.exp2(4.2 * rng.random((N, 8, 1, n))) * rng.random((N, 8, 16, n))).astype(np.int64), 15)
    def low(n, top): return np.minimum((top * rng.random((N, 8, 16, n)) ** rng.choice(np.array([1.0, 2.0, 4.0]), (N, 8, 1, n))).astype(np.int64), top - 1)
    LE = (rng.random((N, 8, W)) < rng.random((N, 8, 1))).astype(np.int64)
    return pack(small(W), low(W, W), LG, LE, small(M), low(M, M), low(K, W), small(K))
def setup_inputs_ends(rng):
    X, F, LG, LE, XL, LF, C, Q = parts(rng); h = W // 2
    def faces(n):
        kind = rng.integers(0, 3, (N, 8, 1, n)); a = 15 * np.where(kind == 2, rng.integers(0, 2, (N, 8, 16, n)), kind)
        near = (rng.random((N, 8, 1, n)) < 0.25) & (np.arange(16)[:, None] == rng.integers(0, 16, (N, 8, 1, n)))
        return np.abs(a - near.astype(np.int64))
    def ends(a, top): return np.where(rng.random(a.shape) < 0.66, top * rng.integers(0, 2, a.shape), a)
    X, XL, Q = faces(W), faces(M), faces(K)
    X[..., 0] = 0; X[..., W - 1] = 0; X[..., 1] = 15; X[..., W - 2] = 15
    X[..., 2] = 0; X[..., 0, 2] = 1; X[..., W - 3] = 0; X[..., 15, W - 3] = 1
    m = rng.random((N, 8, 16, h)) < 0.66; e = (W - 1) * rng.integers(0, 2, m.shape)
    F = np.concatenate([np.where(m, e, F[..., :h]), np.where(m, e, F[..., h:])], axis=-1)
    m = rng.random((N, 8, W)) < 0.66; e = (rng.random((N, 8, W)) < 0.6).astype(np.int64)
    LG = np.where(m, (M - 1) * e, LG); LE = np.where(m, e, LE)
    LG[..., 0] = 0; LE[..., 0] = 0; LG[..., W - 1] = M - 1; LE[..., W - 1] = 1
    LF = ends(LF, M - 1); C = ends(C, W - 1)
    for k in (0, 1, K - 1): Q[..., k] = 15; C[..., k] = (W - 1) * rng.integers(0, 2, (N, 8, 16))
    Q[..., K - 2] = 0; C[..., K - 2] = (W - 1) * rng.integers(0, 2, (N, 8, 16))
    for k in (2, K - 3): Q[..., k] = 0; C[..., :15, k] = 1; C[..., 15, k] = W - 1
    for k, v in ((3, 2), (K - 4, W - 3)): Q[..., k] = 15; C[..., :15, k] = (W - 1) * rng.integers(0, 2, (N, 8, 15)); C[..., 15, k] = v
    return pack(X, F, LG, LE, XL, LF, C, Q)
def setup_inputs_corners(rng):
    X, F, LG, LE, XL, LF, C, Q = parts(rng); cnt = (0, 1, CAP - 1, CAP, CAP + 1, K); a = np.arange(M)
    for g in (2, 7):
        LG[:, g] = LG[0, g]; res = a[(LG[0, g][h1(a)] == a) | (LG[0, g][h2(a)] == a)]; LF[:, g] = rng.choice(res, (N, 16, M))
    v = LG[:, 3]; c = np.arange(W)
    for _ in range(3): v = np.where((h1(v) == c) | (h2(v) == c), (v + 1) % M, v)
    LG[:, 3] = v
    few = np.array([0, 1, M - 2, M - 1]); LF[:, 5] = rng.choice(few, (N, 16, M)); LG[:, 6] = rng.choice(few, (N, W))
    LE[:, 4] = 1; LE[0, 0] = 0
    for q in range(N):
        for g in range(8):
            b = rng.permutation(W)[:4 * K].reshape(K, 4)
            C[q, g] = b[np.arange(K)[None, :], rng.integers(0, 4, (16, K))]
            ask = np.zeros(K, np.int64); ask[rng.permutation(K)[:cnt[(q + g) % 6]]] = 1
            if g == 7:
                o = C[q, g][np.argmin(far(X[q, g], C[q, g], Q[q, g]), axis=0), np.arange(K)]; LE[q, g] = 0; LE[q, g, o] = ask
            else: LE[q, g, b] = ask[:, None]
    return pack(X, F, LG, LE, XL, LF, C, Q)
def setup_inputs_ties(rng):
    X, F, LG, LE, XL, LF, C, Q = parts(rng)
    pal = rng.integers(6, 10, (N, 8, 16, 6))
    X = np.take_along_axis(pal, rng.integers(0, 6, (N, 8, 1, W)), 3); XL = np.take_along_axis(pal, rng.integers(0, 6, (N, 8, 1, M)), 3)
    for q in range(N):
        for g in range(8):
            v = rng.permutation(M)[:M // 2]; LG[q, g, h2(v)] = v; LG[q, g, h1(v)] = v
    return pack(X, F, LG, LE, XL, LF, C, Q)
def setup_inputs_alike(rng):
    X, F, LG, LE, XL, LF, C, Q = parts(rng)
    for g in range(8):
        s = rng.permutation(M); w = s[:64]; pl = np.concatenate([h1(w), h2(w)])
        pair = s[:6]; few = np.concatenate([pair, pair ^ 1])
        for q in range(N):
            if g % 2 == 0:
                pool = rng.permutation(W)[:40]; C[q, g] = rng.choice(pool, (16, K)); F[q, g, :, ::2] = rng.choice(pool, (16, W // 2))
                LE[q, g, pool] = rng.random(40) < 0.8; LG[q, g, pool] = rng.choice(few, 40); LF[q, g] = rng.choice(s[:24], (16, M))
            else:
                C[q, g] = rng.choice(pl, (16, K)); LE[q, g, pl] = 1; LG[q, g, pl] = rng.choice(s[64:], 128); LF[q, g] = rng.choice(w, (16, M))
    return pack(X, F, LG, LE, XL, LF, C, Q)
def check_inputs(d):
    bad = []
    for k, lo, hi in (("xr", 0, 15), ("fd", 0, W * W - 1), ("tg", 0, 2 * M - 1), ("xl", 0, 15), ("lf", 0, M - 1), ("cx", 0, W - 1), ("qx", 0, 15)):
        a = np.asarray(d[k]).astype(np.float64)
        if not (np.min(a) >= lo and np.max(a) <= hi): bad.append("range of " + k)
        elif np.any(a != np.floor(a)): bad.append("whole numbers of " + k)
    return bad
def lowest(key, use):
    ix = np.flatnonzero(use); m = np.zeros(len(key), bool); m[ix[np.unique(key[ix], return_index=True)[1]]] = True
    return m
def far(x, c, q):
    return np.add.reduce(np.abs(x[:, c] - q[:, None, :]), axis=0)
def reference(xr, fd, tg, xl, lf, cx, qx):
    def whole(a): return a.astype(np.float32).astype(np.int64).reshape(N, 8, 16, -1)
    X, XL, Q = whole(xr), whole(xl), whole(qx)
    fi = fd.astype(np.int64); F = np.concatenate([fi & (W - 1), fi >> LW], axis=-1).reshape(N, 8, 16, W)
    LG = tg.astype(np.int64) >> 1; LE = tg.astype(np.int64) & 1; LF = lf.astype(np.int64).reshape(N, 8, 16, M)
    C = np.ascontiguousarray(np.stack([gentries(a) for a in cx]).astype(np.int64).reshape(N, 8, K, 16).transpose(0, 1, 3, 2))
    lane = np.arange(K)
    for t in range(RO):
        asked = {}; back = {}
        for r in range(N):
            for g in range(8):
                c = C[r, g]; o = c[np.argmin(far(X[r, g], c, Q[r, g]), axis=0), lane]
                s = np.flatnonzero(lowest(o, LE[r, g][o] == 1))[:CAP]
                asked[r, g] = (o, s, LG[r, g][o[s]], LG[r, g][c[:, s]])
        for r in range(N):
            p = (r + 1 + t % (N - 1)) % N
            for g in range(8):
                o, s, n, sent = asked[r, g]
                back[r, g] = (XL[p, g][:, n], LF[p, g][:, n])
                w = lowest(n ^ 1, np.ones(len(n), bool)); LF[p, g][:, (n ^ 1)[w]] = sent[:, w]
        for r in range(N):
            for g in range(8):
                o, s, n, sent = asked[r, g]; a, v = back[r, g]; q = Q[r, g][:, s]; j = np.arange(len(s))
                c1, c2 = h1(v), h2(v); in1 = LG[r, g][c1] == v; in2 = LG[r, g][c2] == v
                sh = np.where(in1, c1, np.where(in2, c2, np.where(far(X[r, g], c2, q) > far(X[r, g], c1, q), c2, c1)))
                new = ~(in1 | in2); i = np.argmax(new, axis=0); pl = sh[i, j]; w = lowest(pl, np.any(new, axis=0))
                LG[r, g][pl[w]] = v[i, j][w]; LE[r, g][pl[w]] = 1
                F[r, g][:, o[s]] = sh; X[r, g][:, o[s]] = a; LE[r, g][o[s]] = 0
                C[r, g] = F[r, g][:, o]; Q[r, g] = (Q[r, g] + X[r, g][:, o]) >> 1
    return {"yc": C.reshape(N, 128, K).astype(np.float32), "yq": Q.reshape(N, 128, K).astype(np.float32).astype(BF), "yt": (2 * LG + LE).astype(np.float32), "yl": LF.reshape(N, 128, M).astype(np.float32)}

@@ -1,0 +1,681 @@
+from concourse.bass import DstId, RemoteDMATransfer
+from concourse.mybir import AluOpType as OP, AxisListType, ActivationFunctionType as AF
+
+N, W, M, K, CAP, RO = 6, 2048, 1536, 256, 96, 3
+ON_S, HALF = (1, 3, 5, 7), 64
+DB = (0, 1, 2, 5)
+SEQ = ("g0 g1 d0 h0 g2 d1 a0 h1 g3 d2 a1 h2 d3 a2 g4 g5 d4 a3 g6 k0 d5 a4 g7 d6 a5 d7 a6 a7 h3 k1",
+       "g0 g1 d0 h0 g2 d1 a0 g3 d2 h1 a1 d3 a2 g4 h2 g5 d4 a3 g6 d5 a4 h3 g7 k0 d6 a5 h4 d7 a6 h5 a7 k1")
+WD, MD = W + CAP, M + CAP
+BIG = 16777216.0
+MAGIC = 8388608.0
+DW = 6 + CAP
+
+SCRATCH = {}
+_d = {
+    "float32": dict(m16=16, pm=1, w15=1, cn=1, cv=1, cc=1, cl=1, thrp=256, thr=256, thrc=96, z0=256, z1=256, zz=256, kw=16, d257=16, d256=16,
+                    d2w=6, d15w=6, d2r=96, sl1=96, olf=16, u1=16, u2=16, u3=16, bf=96, bb=192, s1=96, s2=96, c1f=96, dcf=96, sx1=96, sf=96, nl=6,
+                    mn1=6, mn2=6, mn3=6, mn4=6, mn5=6, sp=96, vl=6, vt1=6, vt2=6, vt3=6, zf=512, yl0=MD, ycf=256, ytf=W, zz2=128, cy=1),
+    "bfloat16": dict(ib=128, rr=2048, ones=128, blk=128, sels=8, ckey=128, ki=256, kadd=256, vlo=128, vhb=128, dm=96, deft=96, maskc=96, maskl=96,
+                     woff=128, wdiag=128, tri=128, rv=128, re_=128, rn=128, rk=128, rp=128, lp5=128, wb=144, wbn=144, wbv=144, wbk=144, wb0=144,
+                     wbx=144, wbxn=144, wb2=144, wb2n=144, xw=WD, gw=WD, xlo=M, xl0=M, xl1=M, xl2=M, xc=4096, ab=4096, qq=512, xo=256,
+                     go=256, eq=4096, cc2=512, sw=512, at=96, qe=1536, g1=1536, g2=1536, gs=1536, m1=1536, m2=1536, pr=96, g2f=96, wf=96, chf=96,
+                     e12=192, tmx=96, eqn=576, mfl=96, eqc=576, cfl=96, gvm=96, gn=96, glm=96, gl2=96, gh=128, gl=128, ge=128, one2=256, wyt=8),
+    "float16": dict(ih=128, maskb=256, blk16=8, blkh=128, blkhn=128, trih=128, lp0=128, lp1=128, lp4=128, wbh=144, wbhn=144, c16=256, olm=256, orh=256, nrh=96,
+                    nr=96, f1=96, fv=96, fbh=96, fbl=96, vrh=96),
+    "int32": dict(d1=128, pb=256, kc=256, ca=16, pc=1, vhi=128, d1s=128, pbs=256, vhs=128, pcs=1, cxi=256, cw=256, fdi=1024, fw=WD, tgi=128, th=128,
+                  tl=128, te=128, lfo=M, lf0=MD, lf1=MD, lf2=MD, ks=256, ol=16, ci=192, cm=192, bi=96, bhi=96, blo=96, nli=6, nb=6),
+    "uint16": dict(expl=16, cu=256, olu=16, su=16, nu=6, kru=96, osu=6, klu=6, csu=96, cl12=192, vu=6,
+                   db0=DW, db1=DW, db2=DW, rd10=DW, rd20=DW, rd21=DW, ro0=DW, ro1=DW, ro2=DW),
+}
+_WHERE = {}
+_SOLO = ("xw", "gw", "fw", "xlo", "xl0", "xl1", "xl2", "lfo", "lf0", "lf1", "lf2", "yl0", "sw", "db0", "db1", "db2", "rd10", "rd20", "rd21", "ro0", "ro1", "ro2",
+         "xc", "ab", "cw", "fdi", "cxi", "tgi", "ol", "ytf", "ycf", "cl12")
+for _dt in _d:
+    _small, _at = "pool_" + _dt, 0
+    for _n in _d[_dt]:
+        _c = _d[_dt][_n]
+        if _n in _SOLO:
+            SCRATCH["t_" + _n] = ("sbuf", [128, _c], _dt)
+            _WHERE[_n] = ("t_" + _n, 0, _c)
+        else:
+            _WHERE[_n] = (_small, _at, _c)
+            _at += (_c + 15) // 16 * 16
+    SCRATCH[_small] = ("sbuf", [128, _at], _dt)
+SCRATCH["t_sx"] = ("sbuf", [8, W], "bfloat16")
+for _i in range(8):
+    SCRATCH["p%d" % _i] = ("psum", [128, 512], "float32")
+
+DELTAS = ("rd10", "rd20", "rd21", "ro0", "ro1", "ro2")
+SEMAPHORES = (["sv", "ss", "st", "sg"] + ["D%d" % i for i in range(24)] + ["L%d" % i for i in range(24)]
+              + ["a_lf%d" % i for i in range(3)] + ["a_xl%d" % i for i in range(3)] + ["a_" + n for n in DELTAS])
+
+
+def rank_program(g, core, T, topo):
+    rank = T.rank_of(core)
+    if rank is None:
+        return
+    cores = list(T.cores)
+    eng = {"v": g.vector, "s": g.scalar, "t": g.tensor, "g": g, "y": g.sync}
+    qsem = {"v": "sv", "s": "ss", "t": "st", "g": "sg"}
+    cnt = {"v": 0, "s": 0, "t": 0, "g": 0}
+    know = {q: {} for q in eng}
+    last_w, readers, bank, final, nsem = {}, {}, {}, {}, {"D": 0, "L": 0}
+
+    def wait(q, ev):
+        sem, val, snap = ev[0], ev[1], ev[2]
+        if know[q].get(sem, 0) >= val:
+            return
+        eng[q].wait_ge(T.sem[sem], val)
+        know[q][sem] = val
+        for s in snap:
+            if know[q].get(s, 0) < snap[s]:
+                know[q][s] = snap[s]
+
+    def before(q, R, Wr):
+        for k in R:
+            if k[0] == "#":
+                continue
+            if k in last_w and not (last_w[k][3] == q and q == "t"):
+                wait(q, last_w[k])
+        for k in Wr:
+            if k[0] == "#":
+                continue
+            if k in last_w and not (last_w[k][3] == q and q == "t"):
+                wait(q, last_w[k])
+            for rq in readers.get(k, {}):
+                wait(q, readers[k][rq])
+        for k in set(R) | set(Wr):
+            if k[0] == "#":
+                for oq in bank.get(k, {}):
+                    if oq != q:
+                        wait(q, bank[k][oq])
+
+    def after(q, ev, R, Wr):
+        for k in R:
+            if k[0] != "#":
+                readers.setdefault(k, {})[ev[3]] = ev
+        for k in Wr:
+            if k[0] != "#":
+                last_w[k] = ev
+                readers[k] = {}
+        for k in set(R) | set(Wr):
+            if k[0] == "#":
+                bank.setdefault(k, {})[q] = ev
+
+    def emit(q, R, Wr, call):
+        before(q, R, Wr)
+        ins = call(eng[q])
+        cnt[q] += 1
+        ins.then_inc(T.sem[qsem[q]], 1)
+        final[qsem[q]] = cnt[q]
+        after(q, (qsem[q], cnt[q], dict(know[q]), q), R, Wr)
+
+    def dma(q, out, in_):
+        s = "D%d" % nsem["D"]
+        nsem["D"] += 1
+        R, Wr = keys_in([in_]), [out[1]]
+        before(q, R, Wr)
+        eng[q].dma_start(out[0], in_[0]).then_inc(T.sem[s], 16)
+        final[s] = 16
+        after(q, (s, 16, dict(know[q]), "dma" + s), R, Wr)
+
+    def send(dst, name, cols, src, sem):
+        es = topo.engines(core, dst)
+        if topo.chip(core) == topo.chip(dst):
+            es = es[len(es) // 2:]
+        mask = 0
+        for e in es:
+            mask |= 1 << e
+        rid, pid = topo.addr(dst)[0], topo.addr(dst)[1]
+        s = "L%d" % nsem["L"]
+        nsem["L"] += 1
+        before("g", [src], [])
+        o, a = T["t_" + name], T["t_" + src]
+        g.remote_dma(o[:, 0:cols], a[:, 0:cols], T.sem[sem], T.sem[s], pid, rid, mask)
+        final[s] = len(es)
+        after("g", (s, len(es), dict(know["g"]), "rem" + s), [src], [])
+
+    def arrive(src, name, sem):
+        es = topo.engines(src, core)
+        n = len(es) // 2 if topo.chip(core) == topo.chip(src) else len(es)
+        final[sem] = n
+        last_w[name] = (sem, n, {}, "arr")
+
+    def B(name, lo=0, hi=None, step=1, key=None):
+        b, at, w = _WHERE[name]
+        hi = w if hi is None else hi
+        return (T[b][:, at + lo:at + hi:step] if step > 1 else T[b][:, at + lo:at + hi], key or name, ())
+
+    def P(i, lo, hi, step=1, p0=0, p1=128):
+        t = T["p%d" % i]
+        return (t[p0:p1, lo:hi:step] if step > 1 else t[p0:p1, lo:hi], "#%d" % i, ())
+
+    def I(win, off):
+        return (win[0].indirect(off[0]), win[1], (off[1],))
+
+    def keys_in(ops):
+        return [o[1] for o in ops] + [k for o in ops for k in o[2]]
+
+    def copy(out, in_):
+        emit("v", keys_in([in_]) + list(out[2]), [out[1]], lambda e: e.tensor_copy(out=out[0], in_=in_[0]))
+
+    def tt(out, a, b, op):
+        emit("v", keys_in([a, b]) + list(out[2]), [out[1]], lambda e: e.tensor_tensor(out=out[0], in0=a[0], in1=b[0], op=op))
+
+    def ts(out, a, s1, op0, s2=None, op1=None):
+        x1 = s1[0] if isinstance(s1, tuple) else s1
+        x2 = s2[0] if isinstance(s2, tuple) else s2
+        R = keys_in([x for x in (a, s1, s2) if isinstance(x, tuple)])
+        if op1 is None:
+            emit("v", R, [out[1]], lambda e: e.tensor_scalar(out=out[0], in0=a[0], scalar1=x1, scalar2=None, op0=op0))
+        else:
+            emit("v", R, [out[1]], lambda e: e.tensor_scalar(out=out[0], in0=a[0], scalar1=x1, scalar2=x2, op0=op0, op1=op1))
+
+    def scan(out, d0, d1, init, op0, op1):
+        emit("v", keys_in([d0, d1]), [out[1]], lambda e: e.tensor_tensor_scan(out=out[0], data0=d0[0], data1=d1[0], initial=init, op0=op0, op1=op1))
+
+    def fill(out, c):
+        emit("v", [], [out[1]], lambda e: e.memset(out[0], c))
+
+    def act(out, in_, func, bias=0.0, scale=1.0):
+        emit("s", keys_in([in_]), [out[1]], lambda e: e.activation(out=out[0], in_=in_[0], func=func, bias=bias, scale=scale))
+
+    def mm(out, lhsT, rhs, start, stop):
+        emit("t", keys_in([lhsT, rhs]), [out[1]], lambda e: e.matmul(out[0], lhsT[0], rhs[0], start, stop))
+
+    def iota(out, pattern, base, cm):
+        fl = out[1] in ("ckey", "ki", "vlo", "dm")
+        if fl:
+            emit("g", [], [out[1]], lambda e: e.iota(out[0], pattern, base, cm, allow_small_or_imprecise_dtypes=True))
+        else:
+            emit("g", [], [out[1]], lambda e: e.iota(out[0], pattern, base, cm))
+
+    def wide(name, c):
+        return B(name, 15 - c, 143 - c)
+
+    def wrap(bk, lo, sets, n, start=True, stop=True):
+        tot = len(sets) * 16
+        k = 0
+        for wname, rows, r0 in sets:
+            for c in range(16):
+                mm(P(bk, lo, lo + n), wide(wname, c), B(rows, r0 + c, r0 + 16 * n, 16), start and k == 0, stop and k == tot - 1)
+                k += 1
+
+    def lanes(bk, lo, sets):
+        tot = len(sets) * 16
+        k = 0
+        for wname, src, key in sets:
+            for i in range(16):
+                mm(P(bk, lo, lo + CAP), wide(wname, i), B(src, i, 16 * CAP, 16, key=key), k == 0, k == tot - 1)
+                k += 1
+
+    def X(t, key):
+        return (t, key, ())
+
+    dma("y", B("xw", 0, W), X(T.xr[:], "in"))
+    dma("s", B("cxi"), X(T.cx[:], "in"))
+    dma("s", B("qq", 256, 512, key="qr"), X(T.qx[:], "in"))
+    dma("y", B("lfo"), X(T.lf[:], "in"))
+    dma("s", B("tgi"), X(T.tg[:], "in"))
+    dma("y", B("xlo"), X(T.xl[:], "in"))
+    dma("y", B("fdi"), X(T.fd[:], "in"))
+
+    plan = []
+    for d in range(N):
+        hold = [(d, None)]
+        for t in range(RO):
+            u = (d - 1 - t) % N
+            src = hold[0]
+            for h in hold:
+                if topo.chip(cores[h[0]]) == topo.chip(cores[u]):
+                    src = h
+            plan.append((t, src[0], src[1], u))
+            hold.append((u, t))
+
+    def send_disk(t, own):
+        for (tt_, src, held, u) in plan:
+            if tt_ == t and src == rank and (held is None) == own:
+                send(cores[u], "lf%d" % t, M, "lfo" if held is None else "lf%d" % held, "a_lf%d" % t)
+                send(cores[u], "xl%d" % t, M, "xlo" if held is None else "xl%d" % held, "a_xl%d" % t)
+
+    for (t, src, held, u) in plan:
+        if u == rank:
+            arrive(cores[src], "lf%d" % t, "a_lf%d" % t)
+            arrive(cores[src], "xl%d" % t, "a_xl%d" % t)
+    for n, back in (("rd10", 1), ("rd20", 2), ("rd21", 1)):
+        arrive(cores[(rank + back) % N], n, "a_" + n)
+    for t in range(RO):
+        arrive(cores[(rank - 1 - t) % N], "ro%d" % t, "a_ro%d" % t)
+
+    fill(B("ones"), 1.0)
+    emit("g", ["ones"], ["ib"], lambda e: e.affine_select(B("ib")[0], B("ones")[0], [[1, 128]], OP.is_equal, 0.0, 0, -1))
+    iota(B("d1"), [[16, 8], [0, 16]], 15, -1)
+    iota(B("pb"), [[0, 16], [-1, 16]], 0, 1)
+    iota(B("ckey"), [[0, 8], [16, 16]], 0, 0)
+    iota(B("ca"), [[1, 16]], 0, 0)
+    iota(B("kc"), [[0, 16], [1, 16]], 0, 0)
+    iota(B("ki"), [[1, 256]], 0, 0)
+    iota(B("pc"), [[1, 1]], 0, 1)
+    iota(B("vhi"), [[1, 8], [0, 16]], 0, 8)
+    iota(B("vlo"), [[0, 8], [1, 16]], 0, 0)
+    iota(B("dm"), [[1, 6], [0, 16]], 128, 0)
+    for i in range(16):
+        act(B("rr", i, 2048, 16, key="rr"), B("ib"), AF.Copy, scale=-1.0)
+    for kh in range(2):
+        mm(P(5, 128 * kh, 128 * kh + 128), B("qq", 256 + 128 * kh, 384 + 128 * kh, key="qr"), B("ib"), True, True)
+    act(B("qq", 0, 256, key="qt"), P(5, 0, 256), AF.Copy)
+
+    def consts_a():
+        fill(B("xw", W, WD, key="xwd"), 0.0)
+        copy(B("ih"), B("ib"))
+        ts(B("d1s"), B("d1"), 4, OP.arith_shift_right)
+        ts(B("blk"), B("d1s"), 0.0, OP.is_equal)
+        ts(B("sels"), B("blk", 0, 128, 16), 32768.0, OP.mult)
+        ts(B("pbs"), B("pb"), 15, OP.bitwise_and)
+        ts(B("maskb"), B("pbs"), 0.0, OP.is_equal)
+        ts(B("m16"), B("pbs", 0, 16), 0.0, OP.is_equal)
+        copy(B("blk16"), B("blk", 0, 128, 16))
+        copy(B("expl"), B("ca"))
+        ts(B("zz2"), B("kc", 0, 128), 0.0, OP.is_equal, 2.0 * BIG, OP.mult)
+        fill(B("one2"), 1.0)
+        emit("g", ["blk"], ["tri"], lambda e: e.affine_select(B("tri")[0], B("blk")[0], [[1, 128]], OP.is_gt, 0.0, 0, -1))
+        copy(B("cu"), B("cxi"))
+        copy(B("c16"), B("cu"))
+        fill(B("gw", key="gw"), 0.0)
+
+    def col(f):
+        return B("m16", f, f + 1)
+
+    def consts_g():
+        ts(B("th"), B("tgi"), 5, OP.arith_shift_right)
+        ts(B("tl"), B("tgi"), 1, OP.arith_shift_right, 15, OP.bitwise_and)
+        ts(B("te"), B("tgi"), 1, OP.bitwise_and)
+        ts(B("vhs"), B("vhi"), 127, OP.bitwise_and)
+        copy(B("gh"), B("th"))
+        copy(B("gl"), B("tl"))
+        copy(B("ge"), B("te"))
+        copy(B("vhb"), B("vhs"))
+        for f, n in ((0, "gh"), (1, "gl"), (2, "vhb"), (3, "vlo"), (4, "ge")):
+            before("y", [n], ["gw"])
+            s = "D%d" % nsem["D"]
+            nsem["D"] += 1
+            g.sync.dma_start(T.t_gw[f:128:16, 0:W], B(n)[0]).then_inc(T.sem[s], 16)
+            final[s] = 16
+            last_w["gw%d" % f] = (s, 16, dict(know["y"]), "dma" + s)
+
+    GW = ["gw%d" % f for f in range(6)]
+
+    def consts_b():
+        ts(B("cv"), col(2), 16.0, OP.mult, col(3), OP.add)
+        ts(B("rv"), B("blk"), B("cv"), OP.mult)
+        ts(B("kadd"), B("ki"), col(6), OP.mult)
+        ts(B("re_"), B("blk"), col(4), OP.mult, -BIG, OP.mult)
+        ts(B("woff"), B("blk"), 65536.0, OP.mult)
+        ts(B("zz"), B("kc"), 0.0, OP.is_equal)
+        ts(B("z1"), B("zz"), 65536.0, OP.mult)
+        ts(B("z0"), B("zz"), -0.5, OP.mult, 0.5, OP.add)
+        scan(B("thrp"), B("z0"), B("z1"), 0.0, OP.mult, OP.add)
+        ts(B("thr"), B("thrp"), -BIG, OP.add)
+        tt(B("z0", 0, 16), B("thrp", 0, 16), B("m16"), OP.mult)
+        emit("v", ["z0"], ["w15"], lambda e: e.tensor_reduce(out=B("w15")[0], in_=B("z0", 0, 16)[0], axis=AxisListType.X, op=OP.add))
+        ts(B("wdiag"), B("blk"), B("w15"), OP.mult, 0.5, OP.mult)
+        fill(B("wb"), 0.0)
+        copy(B("wb", 15, 143, 16), B("blk", 0, 128, 16))
+        ts(B("wb0"), B("wb"), col(0), OP.mult)
+        ts(B("cn"), col(0), 16.0, OP.mult, col(1), OP.add)
+        ts(B("wbn"), B("wb"), B("cn"), OP.mult)
+        ts(B("pcs"), B("pc"), 15, OP.bitwise_and)
+        copy(B("pm"), B("pcs"))
+        ts(B("kw"), B("ca"), 16.0, OP.mult, B("pm"), OP.add)
+        ts(B("d257"), B("kw"), 257.0, OP.add)
+        ts(B("d256"), B("kw"), 256.0, OP.add)
+        ts(B("deft"), B("vlo", 0, 96), col(3), OP.mult)
+        ts(B("cc2", 0, 96, key="cc2"), B("dm"), col(2), OP.mult)
+        tt(B("deft"), B("deft"), B("cc2", 0, 96), OP.add)
+
+    def consts_c():
+        ts(B("rk"), B("blk"), col(6), OP.mult)
+        ts(B("wbv"), B("wb"), B("cv"), OP.mult)
+        ts(B("wbk"), B("wb"), col(6), OP.mult)
+        ts(B("rp"), B("blk"), col(4), OP.mult)
+        ts(B("rn"), B("blk"), B("cn"), OP.mult)
+        ts(B("d15w"), B("kw", 0, 6), float(M), OP.add)
+        ts(B("wb2"), B("wb"), 2.0 ** -8, OP.mult)
+        ts(B("wb2n"), B("wb"), -2.0 ** -8, OP.mult)
+        ts(B("wbx"), B("wb"), col(5), OP.mult, 2.0 ** -9, OP.mult)
+        ts(B("wbxn"), B("wb"), col(5), OP.mult, -2.0 ** -9, OP.mult)
+
+    def consts_d():
+        ts(B("d2w"), B("kw", 0, 6), float(W), OP.add)
+        ts(B("d2r"), B("ki", 0, 96), float(W), OP.add)
+        ts(B("sl1"), B("ki", 0, 96), 1024.0, OP.add)
+        ts(B("thrc"), B("thrp", 0, 96), -1024.0, OP.add)
+        copy(B("blkh"), B("blk"))
+        ts(B("blkhn"), B("blk"), -1024.0, OP.mult)
+        copy(B("wbh"), B("wb"))
+        ts(B("wbhn"), B("wb"), -1024.0, OP.mult)
+        for n, f in (("lp0", 0), ("lp1", 1), ("lp4", 4), ("lp5", 5)):
+            fill(B(n), 0.0) if n == "lp5" else ts(B(n), B("blk"), 0.0, OP.mult)
+            copy(B(n, f, 128, 16), B("blk", 0, 128, 16))
+        ts(B("cl"), col(4), -1.0, OP.mult, 1.0, OP.add)
+        tt(B("cc"), B("cl"), col(0), OP.subtract)
+        tt(B("cc"), B("cc"), col(1), OP.subtract)
+        ts(B("maskc"), B("ones", 0, 96), B("cc"), OP.mult)
+        tt(B("cl"), B("cl"), col(5), OP.subtract)
+        ts(B("maskl"), B("ones", 0, 96), B("cl"), OP.mult)
+        copy(B("trih"), B("tri"))
+        ts(B("cy"), B("cn"), 2.0, OP.mult, col(4), OP.add)
+        ts(B("wyt"), B("blk", 0, 128, 16), B("cy"), OP.mult)
+
+    def unpack():
+        fill(B("fw", W, WD, key="fw"), 0)
+        copy(B("cw"), B("cxi"))
+        ts(B("fw", 0, 1024, key="fwa"), B("fdi"), 2047, OP.bitwise_and)
+        ts(B("fw", 1024, 2048, key="fwb"), B("fdi"), 11, OP.arith_shift_right)
+
+    def sums_of_x():
+        for m in range(4):
+            mm(P(6 + m % 2, 0, 512, p1=8), B("blk", 0, 128, 16), B("xw", 512 * m, 512 * m + 512), True, True)
+            emit("s", ["#%d" % (6 + m % 2)], ["sx"], lambda e: e.activation(out=T.t_sx[:, 512 * m:512 * m + 512], in_=P(6 + m % 2, 0, 512, p1=8)[0], func=AF.Copy))
+        before("y", ["sx"], ["gw"])
+        s = "D%d" % nsem["D"]
+        nsem["D"] += 1
+        g.sync.dma_start(T.t_gw[5:128:16, 0:W], T.t_sx[:]).then_inc(T.sem[s], 16)
+        final[s] = 16
+        last_w["gw5"] = (s, 16, dict(know["y"]), "dma" + s)
+
+    def gwin():
+        b = B("gw")
+        return (b[0], "gw", tuple(GW))
+
+    def IG(off):
+        b = B("gw")
+        return (b[0].indirect(off[0]), "gw", tuple(GW) + (off[1],))
+
+    def IX(off):
+        b = B("xw")
+        return (b[0].indirect(off[0]), "xw", ("xwd", off[1]))
+
+    def IF(off):
+        b = B("fw")
+        return (b[0].indirect(off[0]), "fw", ("fwa", "fwb", off[1]))
+
+    def eqs(tile, rows, n, cols, wd, bk, lo, width):
+        for j in range(n):
+            k = "%s%d" % (tile, j)
+            ts(B(tile, width * j + 16 * j, width * j + width, key=k), B(rows, 16 * j, width), B(cols, j, j + 1), OP.is_equal)
+            if j < n - 1:
+                mm(P(bk, lo + 16 * (j + 1), lo + width), B("woff"), B(tile, width * j + 16 * (j + 1), width * j + width, key=k), False, False)
+            mm(P(bk, lo + 16 * j, lo + 16 * j + 16), B("wdiag"), B(tile, width * j + 16 * j, width * j + 16 * j + 16, key=k), False, j == n - 1)
+
+    def choice(t, hooks):
+        def gather(j):
+            o, i_ = B("xc", 512 * j, 512 * j + 512, key="xc%d" % j), IX(B("cu", 32 * j, 32 * j + 32))
+            if j in ON_S:
+                act(o, i_, AF.Copy)
+            else:
+                copy(o, i_)
+
+        def differ(j):
+            bk, kh, jj = DB[j % 4], j // 4, j % 4
+            mm(P(bk, 0, 512), B("ib"), B("xc", 512 * j, 512 * j + 512, key="xc%d" % j), True, False)
+            mm(P(bk, 0, 512), B("qq", 128 * kh, 128 * kh + 128, key="qt"), B("rr", 512 * jj, 512 * jj + 512, key="rr"), False, True)
+
+        def dist(j):
+            act(B("ab", 512 * j, 512 * j + 512, key="ab%d" % j), P(DB[j % 4], 0, 512), AF.Abs)
+
+        def keys(kh):
+            kb = 3 + kh
+            mm(P(kb, 0, 128), B("c16", 128 * kh, 128 * kh + 128), B("ih"), True, False)
+            mm(P(kb, 0, 128), B("ones"), B("ckey"), False, False)
+            for i in range(16):
+                o, a, r = P(kb, i, 128, 16), B("ab", 2048 * kh + i, 2048 * kh + 2048, 16), B("sels")
+                emit("t", ["sels"] + ["ab%d" % j for j in range(4 * kh, 4 * kh + 4)], [o[1]], lambda e: e.matmul(o[0], a[0], r[0], False, i == 15))
+
+        does = {"g": gather, "d": differ, "a": dist, "k": keys}
+        for tok in SEQ[t > 0].split():
+            if tok[0] == "h":
+                for h in hooks.get(int(tok[1:]), []):
+                    h()
+            else:
+                does[tok[0]](int(tok[1:]))
+        for kh in range(2):
+            scan(B("ks", 128 * kh, 128 * kh + 128, key="ks%d" % kh), B("zz2"), P(3 + kh, 0, 128), 0.0, OP.add, OP.min)
+        emit("v", ["ks0", "ks1"], ["ol"], lambda e: e.tensor_scalar(out=B("ol")[0], in0=B("ks", 15, 256, 16)[0], scalar1=2047, scalar2=None, op0=OP.bitwise_and))
+        tt(B("olm"), I(B("ol"), B("expl")), B("maskb"), OP.mult)
+        for kh in range(2):
+            mm(P(6, 8 * kh, 8 * kh + 8), B("olm", 128 * kh, 128 * kh + 128), B("blk16"), True, True)
+        copy(B("olu"), P(6, 0, 16))
+        copy(B("olf"), P(6, 0, 16))
+        tt(B("go"), IG(B("olu")), B("kadd"), OP.add)
+        mm(P(7, 0, 256), B("rv"), B("go"), True, True)
+        mm(P(5, 0, 256), B("re_"), B("go"), True, False)
+
+    def requests(t, fillers):
+        copy(B("orh"), P(7, 0, 256))
+        eqs("eq", "orh", 16, "olf", None, 5, 0, 256)
+        copy(B("sw", 0, 96), B("deft"))
+        tt(B("cc2", 0, 256), P(5, 0, 256), B("thr"), OP.is_lt)
+        scan(B("cc2", 256, 512, key="cs"), B("one2"), B("cc2", 0, 256), 0.0, OP.mult, OP.add)
+        for f in fillers[0]:
+            f()
+        for c in range(16):
+            l, r = wide("wb0", c), B("cc2", c, 512, 16)
+            emit("t", ["wb0", "cc2", "cs"], ["#6"], lambda e: e.matmul(P(6, 64, 96)[0], l[0], r[0], c == 0, c == 15))
+        tt(B("u1"), P(6, 80, 96), B("d257"), OP.subtract)
+        tt(B("u2"), B("u1"), P(6, 64, 80), OP.mult)
+        tt(B("u3"), B("u2"), B("d256"), OP.add)
+        copy(B("su"), B("u3"))
+        copy(I(B("sw"), B("su")), B("go"))
+        wrap(0, 0, [("wbn", "sw", 0)], 6)
+        mm(P(1, 0, 96), B("rk"), B("sw", 0, 96), True, True)
+        wrap(2, 0, [("wbk", "sw", 0)], 6)
+        wrap(2, 16, [("wbv", "sw", 0)], 6)
+        mm(P(2, 32, 128), B("rn"), B("sw", 0, 96), True, True)
+        mm(P(2, 128, 224), B("rp"), B("sw", 0, 96), True, True)
+        mm(P(7, 0, 96), B("re_"), B("sw", 0, 96), True, False)
+        for f in fillers[1]:
+            f()
+        copy(B("nu"), P(0, 0, 6))
+        copy(B("bf"), I(B("lf%d" % t, 0, M), B("nu")))
+        act(B("s1"), B("bf"), AF.Square, bias=8.0, scale=2.0)
+        act(B("s2"), B("bf"), AF.Square, bias=592.0)
+        copy(B("kru"), P(1, 0, 96))
+        act(B("qe"), (T[_WHERE["qq"][0]][:, _WHERE["qq"][1] + 256:_WHERE["qq"][1] + 512].indirect(B("kru")[0]), "qr", ("kru",)), AF.Copy)
+        ts(B("ci", 0, 96, key="cia"), B("s1"), 32.0 * 2046, OP.add)
+        ts(B("ci", 96, 192, key="cib"), B("s2"), 32.0 * 1337, OP.add)
+        emit("v", ["cia", "cib"], ["cm"], lambda e: e.tensor_scalar(out=B("cm")[0], in0=B("ci")[0], scalar1=5, scalar2=2047, op0=OP.arith_shift_right, op1=OP.bitwise_and))
+        copy(B("cl12"), B("cm"))
+
+    def later_lists(t):
+        copy(B("klu"), P(2, 0, 6))
+        copy(B("osu"), P(2, 16, 22))
+        copy(B("nrh"), P(2, 32, 128))
+        copy(B("pr"), P(2, 128, 224))
+        copy(B("nl"), P(0, 0, 6))
+        copy(B("csu"), I(B("cw"), B("klu")))
+
+    def dedupe_n(t):
+        eqs("eqn", "nrh", 6, "nl", None, 7, 0, 96)
+
+    def dedupe_n2(t):
+        tt(B("mfl"), P(7, 0, 96), B("thr", 0, 96), OP.is_lt)
+        wrap(7, 128, [("wb0", "mfl", 0)], 6)
+        copy(B("nli"), B("nl"))
+        ts(B("nb"), B("nli"), 1, OP.bitwise_and)
+        ts(B("mn1"), B("nb"), -2.0, OP.mult, 1.0, OP.add)
+        tt(B("mn2"), B("mn1"), B("nl"), OP.add)
+        tt(B("mn3"), B("mn2"), B("d15w"), OP.subtract)
+        tt(B("mn4"), B("mn3"), P(7, 128, 134), OP.mult)
+        tt(B("mn5"), B("mn4"), B("d15w"), OP.add)
+        copy(B("db%d" % t, 0, 6, key="dba%d" % t), B("mn5"))
+
+    def long_names(t):
+        act(B("gs"), IG(B("csu")), AF.Copy)
+        lanes(6, 400, [("wbn", "gs", "gs")])
+
+    def send_delta(t):
+        copy(B("db%d" % t, 6, DW, key="dbb%d" % t), P(6, 400, 496))
+        last_w["db%d" % t] = last_w["dbb%d" % t]
+        wait("g", last_w["dba%d" % t])
+        for k, (back, name) in enumerate({0: ((1, "rd10"), (2, "rd20")), 1: ((1, "rd21"),), 2: ()}[t]):
+            send(cores[(rank - back) % N], name, DW, "db%d" % t, "a_" + name)
+        send(cores[(rank + 1 + t) % N], "ro%d" % t, DW, "db%d" % t, "a_ro%d" % t)
+
+    def apply(dst, src):
+        copy(I(B(dst), B(src, 0, 6)), B(src, 6, DW))
+
+    def translate(t, fillers):
+        tt(B("m1"), IX(B("cl12", 0, 96)), B("qe"), OP.max)
+        act(B("g1"), IG(B("cl12", 0, 96)), AF.Copy)
+        lanes(4, 0, [("wbn", "g1", "g1")])
+        def part(wname, src, lo, hi, key, start=False, stop=False):
+            for i in range(16):
+                mm(P(3, lo, hi), wide(wname, i), B(src, 16 * lo + i, 16 * hi, 16, key=key), start and i == 0, stop and i == 15)
+        part("wb2n", "m1", 0, 96, "m1", start=True)
+        part("wbx", "g1", 0, 96, "g1")
+        H = HALF
+        act(B("at"), I(B("xl%d" % t), B("nu")), AF.Copy)
+        tt(B("m2", 0, 16 * H, key="m2a"), IX(B("cl12", 96, 96 + H)), B("qe", 0, 16 * H), OP.max)
+        act(B("g2", 0, 16 * H, key="g2a"), IG(B("cl12", 96, 96 + H)), AF.Copy)
+        act(B("g2", 16 * H, 1536, key="g2b"), IG(B("cl12", 96 + H, 192)), AF.Copy)
+        tt(B("m2", 16 * H, 1536, key="m2b"), IX(B("cl12", 96 + H, 192)), B("qe", 16 * H, 1536), OP.max)
+        part("wb2", "m2", 0, H, "m2a")
+        part("wbxn", "g2", 0, H, "g2a")
+        for lo, hi, key in ((0, H, "g2a"), (H, 96, "g2b")):
+            for i in range(16):
+                mm(P(4, 96 + lo, 96 + hi), wide("wbn", i), B("g2", 16 * lo + i, 16 * hi, 16, key=key), i == 0, i == 15)
+        part("wbxn", "g2", H, 96, "g2b")
+        part("wb2", "m2", H, 96, "m2b", stop=True)
+        long_names(t)
+        copy(B("bb", 0, 96, key="bba"), B("bf"))
+        copy(B("bb", 96, 192, key="bbb"), B("bf"))
+        copy(B("c1f"), B("cm", 0, 96))
+        tt(B("dcf"), B("cm", 96, 192), B("cm", 0, 96), OP.subtract)
+        copy((B("xw")[0].indirect(B("osu")[0]), "xw", ("xwd", "osu")), B("at"))
+        copy(B("bi"), B("bf"))
+        ts(B("bhi"), B("bi"), 4, OP.arith_shift_right)
+        ts(B("blo"), B("bi"), 15, OP.bitwise_and)
+        for f in fillers[2]:
+            f()
+        emit("v", ["#4", "bba", "bbb"], ["e12"], lambda e: e.tensor_tensor(out=B("e12")[0], in0=P(4, 0, 192)[0], in1=B("bb")[0], op=OP.is_equal))
+        tt(B("wf"), P(3, 0, 96), B("e12", 96, 192), OP.max)
+        tt(B("chf"), B("wf"), B("e12", 0, 96), OP.is_gt)
+        tt(B("sx1"), B("chf"), B("dcf"), OP.mult)
+        tt(B("sf"), B("sx1"), B("c1f"), OP.add)
+        copy((B("fw")[0].indirect(B("osu")[0]), "fw", ("fwa", "fwb", "osu")), B("sf"))
+
+    def moves(t):
+        last = t == RO - 1
+        copy(B("ycf") if last else B("cu"), IF(B("olu")))
+        act(B("xo"), IX(B("olu")), AF.Identity, bias=-0.5)
+        halves = ((256, 512, "qr"),) if last else ((0, 256, "qt"), (256, 512, "qr"))
+        for lo, hi, key in halves:
+            if key == "qt":
+                for kh in range(2):
+                    o = P(5, 128 * kh, 128 * kh + 128)
+                    mm(o, B("xo", 128 * kh, 128 * kh + 128), B("ib"), True, False)
+                    mm(o, B("qq", 256 + 128 * kh, 384 + 128 * kh, key="qr"), B("ib"), False, True)
+            else:
+                mm(P(5, 256, 512), B("ib"), B("xo"), True, False)
+                mm(P(5, 256, 512), B("ib"), B("qq", 256, 512, key="qr"), False, True)
+        for lo, hi, key in halves:
+            act(B("zf", lo, hi, key="zf" + key), P(5, lo, hi), AF.Identity, scale=0.5, bias=MAGIC)
+            act(B("qq", lo, hi, key=key), B("zf", lo, hi, key="zf" + key), AF.Identity, bias=-MAGIC)
+        if not last:
+            copy(B("c16"), B("cu"))
+
+    def claims(t):
+        def c0():
+            if t < RO - 1:
+                copy(B("cw"), B("cu"))
+            tt(B("tmx"), B("e12", 0, 96), B("e12", 96, 192), OP.max)
+            tt(B("nr"), B("pr"), B("tmx"), OP.is_gt)
+            mm(P(6, 128, 224), B("trih"), B("nr"), True, True)
+            tt(B("sp"), B("sf"), B("sl1"), OP.subtract)
+
+        def c1():
+            tt(B("f1"), B("nr"), P(6, 128, 224), OP.is_gt)
+            tt(B("fv"), B("f1"), B("sp"), OP.mult)
+            wrap(6, 256, [("wbh", "fv", 0), ("wbhn", "f1", 0)], 6)
+            mm(P(6, 288, 384), B("blkh"), B("fv"), True, False)
+            mm(P(6, 288, 384), B("blkhn"), B("f1"), False, True)
+            mm(P(7, 256, 352), B("blkhn"), B("f1"), True, False)
+            tt(B("fbh"), B("f1"), B("bhi"), OP.mult)
+            tt(B("fbl"), B("f1"), B("blo"), OP.mult)
+
+        def c2():
+            tt(B("vl"), P(6, 256, 262), B("d2w"), OP.add)
+            tt(B("vrh"), P(6, 288, 384), B("d2r"), OP.add)
+            eqs("eqc", "vrh", 6, "vl", None, 7, 256, 96)
+
+        def c3():
+            tt(B("cfl"), P(7, 256, 352), B("thrc"), OP.is_lt)
+            wrap(6, 272, [("wb0", "cfl", 0)], 6)
+            mm(P(7, 384, 480), B("lp0"), B("fbh"), True, False)
+            mm(P(7, 384, 480), B("lp1"), B("fbl"), False, False)
+            mm(P(7, 384, 480), B("lp4"), B("f1"), False, True)
+            mm(P(7, 128, 224), B("lp5"), B("at"), True, True)
+            tt(B("vt1"), B("vl"), B("d2w"), OP.subtract)
+
+        def c4():
+            tt(B("vt2"), B("vt1"), P(6, 272, 278), OP.mult)
+            tt(B("vt3"), B("vt2"), B("d2w"), OP.add)
+            copy(B("vu"), B("vt3"))
+            tt(B("gvm"), IG(B("vu")), B("maskc"), OP.mult)
+            tt(B("gn"), B("gvm"), P(7, 384, 480), OP.add)
+            copy((B("gw")[0].indirect(B("vu")[0]), "gw", tuple(GW) + ("vu",)), B("gn"))
+
+        def c5():
+            tt(B("glm"), IG(B("osu")), B("maskl"), OP.mult)
+            tt(B("gl2"), B("glm"), P(7, 128, 224), OP.add)
+            copy((B("gw")[0].indirect(B("osu")[0]), "gw", tuple(GW) + ("osu",)), B("gl2"))
+        return [c0, c1, c2, c3, c4, c5]
+
+    consts_a()
+    send_disk(0, True)
+    hooks = {1: [consts_g], 2: [consts_b, sums_of_x], 3: [unpack]}
+    for t in range(RO):
+        choice(t, hooks)
+        if t == 0:
+            send_disk(1, True)
+            send_disk(1, False)
+            send_disk(2, True)
+            fillers = [[consts_c], [], [consts_d]]
+        elif t == 1:
+            fillers = [[], [lambda: apply("lf1", "rd10")], [lambda: copy(B("yl0", 0, M), B("lfo"))]]
+        else:
+            fillers = [[lambda: apply("lf2", "rd20")], [lambda: apply("lf2", "rd21")], [lambda: apply("yl0", "ro0"), lambda: apply("yl0", "ro1")]]
+        requests(t, fillers)
+        later_lists(t)
+        dedupe_n(t)
+        dedupe_n2(t)
+        translate(t, fillers)
+        moves(t)
+        cl = claims(t)
+        if t < RO - 1:
+            tp = [t]
+            hooks = {0: [lambda: send_delta(tp[0]), cl[0]], 1: [cl[1]], 2: [cl[2]], 3: [cl[3]], 4: [cl[4]], 5: [cl[5]]}
+            if t == 0:
+                hooks[0].append(lambda: send_disk(2, False))
+        else:
+            send_delta(t)
+            dma("y", X(T.yc[:], "yc"), B("ycf"))
+            dma("y", X(T.yq[:], "yq"), B("qq", 256, 512, key="qr"))
+            for c in cl[:5]:
+                c()
+            apply("yl0", "ro2")
+            dma("y", X(T.yl[:], "yl"), B("yl0", 0, M))
+            cl[5]()
+            for m in range(4):
+                emit("t", ["wyt", "gw"], ["#%d" % m], lambda e: e.matmul(P(m, 0, 512, p1=8)[0], B("wyt")[0], B("gw", 512 * m, 512 * m + 512)[0], True, True))
+                o = T.t_ytf[0:8, 512 * m:512 * m + 512]
+                if m % 2:
+                    emit("s", ["#%d" % m], ["ytf%d" % m], lambda e: e.activation(out=o, in_=P(m, 0, 512, p1=8)[0], func=AF.Copy))
+                else:
+                    emit("v", ["#%d" % m], ["ytf%d" % m], lambda e: e.tensor_copy(out=o, in_=P(m, 0, 512, p1=8)[0]))
+            dma("y", X(T.yt[:], "yt"), (T.t_ytf[0:8, :], "ytf0", ("ytf1", "ytf2", "ytf3")))
+    for s in sorted(final):
+        if know["g"].get(s, 0) < final[s]:
+            g.wait_ge(T.sem[s], final[s])

@@ -2,53 +2,106 @@ from concourse.bass import DstId, RemoteDMATransfer
 from concourse.mybir import AluOpType as OP, AxisListType, ActivationFunctionType as AF
 
 N, W, M, K, CAP, RO = 6, 2048, 1536, 256, 96, 3
-ON_S, HALF = (1, 3, 5, 7), 64
-DB = (0, 1, 2, 5)
-SEQ = ("g0 g1 d0 h0 g2 d1 a0 h1 g3 d2 a1 h2 d3 a2 g4 g5 d4 a3 g6 k0 d5 a4 g7 d6 a5 d7 a6 a7 h3 k1",
-       "g0 g1 d0 h0 g2 d1 a0 g3 d2 h1 a1 d3 a2 g4 h2 g5 d4 a3 g6 d5 a4 h3 g7 k0 d6 a5 h4 d7 a6 h5 a7 k1")
+KD = K + 16
 WD, MD = W + CAP, M + CAP
 BIG = 16777216.0
-MAGIC = 8388608.0
+FAR = 8192.0
 DW = 6 + CAP
+DB = (0, 1, 2)
+HALF = 64
+ON_V = 2
+CY, PE, GA, SC, OWN, HOP, DMA0, DMA1, REM, REM0, REM1 = 0.9e-3, 0.46e-3, 1.56, 3.8, 0.06, 0.1, 1.6, 250e3, 0.4, 1.7, 60e3
+KEEP, ROUNDS = 0.3, 6
+ORDER = []
 
 SCRATCH = {}
 _d = {
-    "float32": dict(m16=16, pm=1, w15=1, cn=1, cv=1, cc=1, cl=1, thrp=256, thr=256, thrc=96, z0=256, z1=256, zz=256, kw=16, d257=16, d256=16,
-                    d2w=6, d15w=6, d2r=96, sl1=96, olf=16, u1=16, u2=16, u3=16, bf=96, bb=192, s1=96, s2=96, c1f=96, dcf=96, sx1=96, sf=96, nl=6,
-                    mn1=6, mn2=6, mn3=6, mn4=6, mn5=6, sp=96, vl=6, vt1=6, vt2=6, vt3=6, zf=512, yl0=MD, ycf=256, ytf=W, zz2=128, cy=1),
-    "bfloat16": dict(ib=128, rr=2048, ones=128, blk=128, sels=8, ckey=128, ki=256, kadd=256, vlo=128, vhb=128, dm=96, deft=96, maskc=96, maskl=96,
-                     woff=128, wdiag=128, tri=128, rv=128, re_=128, rn=128, rk=128, rp=128, lp5=128, wb=144, wbn=144, wbv=144, wbk=144, wb0=144,
-                     wbx=144, wbxn=144, wb2=144, wb2n=144, xw=WD, gw=WD, xlo=M, xl0=M, xl1=M, xl2=M, xc=4096, ab=4096, qq=512, xo=256,
-                     go=256, eq=4096, cc2=512, sw=512, at=96, qe=1536, g1=1536, g2=1536, gs=1536, m1=1536, m2=1536, pr=96, g2f=96, wf=96, chf=96,
-                     e12=192, tmx=96, eqn=576, mfl=96, eqc=576, cfl=96, gvm=96, gn=96, glm=96, gl2=96, gh=128, gl=128, ge=128, one2=256, wyt=8),
-    "float16": dict(ih=128, maskb=256, blk16=8, blkh=128, blkhn=128, trih=128, lp0=128, lp1=128, lp4=128, wbh=144, wbhn=144, c16=256, olm=256, orh=256, nrh=96,
-                    nr=96, f1=96, fv=96, fbh=96, fbl=96, vrh=96),
-    "int32": dict(d1=128, pb=256, kc=256, ca=16, pc=1, vhi=128, d1s=128, pbs=256, vhs=128, pcs=1, cxi=256, cw=256, fdi=1024, fw=WD, tgi=128, th=128,
-                  tl=128, te=128, lfo=M, lf0=MD, lf1=MD, lf2=MD, ks=256, ol=16, ci=192, cm=192, bi=96, bhi=96, blo=96, nli=6, nb=6),
-    "uint16": dict(expl=16, cu=256, olu=16, su=16, nu=6, kru=96, osu=6, klu=6, csu=96, cl12=192, vu=6,
-                   db0=DW, db1=DW, db2=DW, rd10=DW, rd20=DW, rd21=DW, ro0=DW, ro1=DW, ro2=DW),
+    "float32": dict(m16=16, pm=1, pw=1, w15=1, cn=1, cv=1, cy=1, cz=1, cg=1, ck=1, ns=1, nb=1, nw=1, top=1, ld0=1, ld1=1, ld2=1, thr=256, z0=256, z1=16, zz=256,
+                    kw=16, kh5=16, dw=6, dw1=6, dm=6, olf=16, acc=8, ball=KD, bf=96, s1=96, s2=96, dcf=96, sf=96, nl=6, vl=6, u1=6, u2=6, u3=6, u4=6,
+                    yl0=MD, ycf=256, ytf=128, zz2=128),
+    "bfloat16": dict(ib=128, imt=128, rr=2048, ones=256, blk=128, sels=8, ckey=128, vlo=128, vhi=128, wdiag=128, tri=128, re_=128,
+                     rn=128, rp=128, bneg=128, lp01=128, lp5=128, ml=128, mc0=128, mc1=128, mc2=128,
+                     wb=144, wbn=144, wbv=144, wbf=144, wby=144, wbx=144, wbxn=144, wb2=144, wb2n=144, xw=WD, gw=WD, xlo=M, xc=4096, ab=4096,
+                     qt=256, qr=KD, xo=256, go=KD, eq=4096, cand=256, cs=256, junk=1536, sw=96, at=96, qc=96, qe=1536, g1=1536, g2=1536, gs=1536,
+                     m1=1536, m2=1536, wf=96, e1=96, e2=96, eqn=576, lsn=96, eqc=576, lsc=96, nr=96, f1=96, fb0=96, old=96, gn=96, gl=96,
+                     p0=128, p1=128, pe=128, px=128, sa=256, ra0=KD, ra1=KD, ra2=KD, yqb=256),
+    "float16": dict(ih=128, maskb=128, blk16=8, blkh=128, lp1h=128, wbh=144, wbmh=144, c16=256, olm=256, ole=256, orh=256, nrh=96, nh=96, fv=96, fb=96, vrh=96),
+    "int32": dict(d1=128, pb=128, kc=256, ca=16, pc=1, d1s=128, pbs=128, pcs=1, vhs=128, vht=128, cxi=256, cw=KD, fdi=1024, fw=WD, tgi=128, tl=128, te=128,
+                  lfo=MD, ks=256, ol=16, ci=192, cm=192),
+    "uint16": dict(expl=16, cu=256, olu=16, nlu=16, klu=6, osu=6, csu=96, cl12=192, vu=6, sb=256, db=DW,
+                   rq0=16, rq1=16, rq2=16, rb0=256, rb1=256, rb2=256, rd0=DW, rd1=DW, rd2=DW),
 }
 _WHERE = {}
-_SOLO = ("xw", "gw", "fw", "xlo", "xl0", "xl1", "xl2", "lfo", "lf0", "lf1", "lf2", "yl0", "sw", "db0", "db1", "db2", "rd10", "rd20", "rd21", "ro0", "ro1", "ro2",
-         "xc", "ab", "cw", "fdi", "cxi", "tgi", "ol", "ytf", "ycf", "cl12")
+_SOLO = ("xw", "gw", "fw", "xlo", "lfo", "yl0", "xc", "ab", "cw", "fdi", "cxi", "tgi", "ol", "ytf", "ycf", "cl12", "qr", "go", "ball", "nlu", "sb", "sa", "db",
+         "rq0", "rq1", "rq2", "rb0", "rb1", "rb2", "ra0", "ra1", "ra2", "rd0", "rd1", "rd2")
 for _dt in _d:
-    _small, _at = "pool_" + _dt, 0
+    _small, _at, _by = "pool_" + _dt, 0, 4 if _dt.endswith("32") else 2
     for _n in _d[_dt]:
         _c = _d[_dt][_n]
         if _n in _SOLO:
             SCRATCH["t_" + _n] = ("sbuf", [128, _c], _dt)
-            _WHERE[_n] = ("t_" + _n, 0, _c)
+            _WHERE[_n] = ("t_" + _n, 0, _c, _by)
         else:
-            _WHERE[_n] = (_small, _at, _c)
+            _WHERE[_n] = (_small, _at, _c, _by)
             _at += (_c + 15) // 16 * 16
     SCRATCH[_small] = ("sbuf", [128, _at], _dt)
-SCRATCH["t_sx"] = ("sbuf", [8, W], "bfloat16")
 for _i in range(8):
     SCRATCH["p%d" % _i] = ("psum", [128, 512], "float32")
 
-DELTAS = ("rd10", "rd20", "rd21", "ro0", "ro1", "ro2")
-SEMAPHORES = (["sv", "ss", "st", "sg"] + ["D%d" % i for i in range(24)] + ["L%d" % i for i in range(24)]
-              + ["a_lf%d" % i for i in range(3)] + ["a_xl%d" % i for i in range(3)] + ["a_" + n for n in DELTAS])
+SEMAPHORES = (["sv", "ss", "st", "sg"] + ["D%d" % i for i in range(24)] + ["L%d" % i for i in range(12)]
+              + ["a_%s%d" % (n, i) for n in ("rq", "rb", "ra", "rd") for i in range(RO)])
+
+
+def in_order(calls):
+    pred, writer, readers = [], {}, {}
+    for n, (ways, R, Wr) in enumerate(calls):
+        p = set(writer[k] for k in R + Wr if k in writer)
+        for k in Wr:
+            p.update(readers.get(k, ()))
+        for k in R:
+            readers.setdefault(k, []).append(n)
+        for k in Wr:
+            writer[k], readers[k] = n, []
+        p.discard(n)
+        pred.append(sorted(p))
+    succ = [[] for _ in calls]
+    for n in range(len(calls)):
+        for p in pred[n]:
+            succ[p].append(n)
+
+    def place(order, needs, back):
+        busy, placed = {}, {}
+        for n in order:
+            best = None
+            for w in calls[n][0]:
+                lead = w[2] - w[1] if back else 0.0
+                at = lead
+                for p in needs[n]:
+                    end, pw = placed[p]
+                    at = max(at, end + lead + (HOP if pw[0] != w[0] else 0.001 if w[0] == "t" else OWN))
+                for a, b in busy.get(w[0], ()):
+                    if at + w[1] <= a:
+                        break
+                    at = max(at, b)
+                end = at - lead + w[2]
+                if best is None or end + (KEEP if w[0] == "v" else 0.0) < best[0]:
+                    best = (end + (KEEP if w[0] == "v" else 0.0), end, at, w)
+            placed[n] = (best[1], best[3])
+            if best[3][1] > 0:
+                busy.setdefault(best[3][0], []).append((best[2], best[2] + best[3][1]))
+                busy[best[3][0]].sort()
+        return placed
+
+    every = range(len(calls))
+    order, best = list(every), None
+    for _ in range(ROUNDS):
+        back = place(order[::-1], succ, True)
+        ahead = place(sorted(every, key=lambda i: (-back[i][0], i)), pred, False)
+        order = sorted(every, key=lambda i: (ahead[i][0], i))
+        if best is None or ahead[order[-1]][0] < best[0]:
+            best = (ahead[order[-1]][0], ahead)
+    ahead = best[1]
+    return [(n, calls[n][0].index(ahead[n][1])) for n in sorted(every, key=lambda i: (ahead[i][0] - ahead[i][1][2], i))]
 
 
 def rank_program(g, core, T, topo):
@@ -60,7 +113,7 @@ def rank_program(g, core, T, topo):
     qsem = {"v": "sv", "s": "ss", "t": "st", "g": "sg"}
     cnt = {"v": 0, "s": 0, "t": 0, "g": 0}
     know = {q: {} for q in eng}
-    last_w, readers, bank, final, nsem = {}, {}, {}, {}, {"D": 0, "L": 0}
+    calls, last_w, readers, bank, final, nsem = [], {}, {}, {}, {}, {"D": 0, "L": 0}
 
     def wait(q, ev):
         sem, val, snap = ev[0], ev[1], ev[2]
@@ -73,609 +126,486 @@ def rank_program(g, core, T, topo):
                 know[q][s] = snap[s]
 
     def before(q, R, Wr):
-        for k in R:
-            if k[0] == "#":
-                continue
+        for k in R + Wr:
             if k in last_w and not (last_w[k][3] == q and q == "t"):
                 wait(q, last_w[k])
         for k in Wr:
-            if k[0] == "#":
-                continue
-            if k in last_w and not (last_w[k][3] == q and q == "t"):
-                wait(q, last_w[k])
             for rq in readers.get(k, {}):
                 wait(q, readers[k][rq])
-        for k in set(R) | set(Wr):
-            if k[0] == "#":
-                for oq in bank.get(k, {}):
-                    if oq != q:
-                        wait(q, bank[k][oq])
-
-    def after(q, ev, R, Wr):
         for k in R:
-            if k[0] != "#":
-                readers.setdefault(k, {})[ev[3]] = ev
-        for k in Wr:
-            if k[0] != "#":
-                last_w[k] = ev
-                readers[k] = {}
-        for k in set(R) | set(Wr):
             if k[0] == "#":
-                bank.setdefault(k, {})[q] = ev
+                for rq in readers.get(k, {}):
+                    if rq != q:
+                        wait(q, readers[k][rq])
 
-    def emit(q, R, Wr, call):
-        before(q, R, Wr)
-        ins = call(eng[q])
-        cnt[q] += 1
-        ins.then_inc(T.sem[qsem[q]], 1)
-        final[qsem[q]] = cnt[q]
-        after(q, (qsem[q], cnt[q], dict(know[q]), q), R, Wr)
+    def after(ev, R, Wr):
+        for k in R:
+            readers.setdefault(k, {})[ev[3]] = ev
+        for k in Wr:
+            last_w[k] = ev
+            readers[k] = {}
 
-    def dma(q, out, in_):
-        s = "D%d" % nsem["D"]
-        nsem["D"] += 1
-        R, Wr = keys_in([in_]), [out[1]]
-        before(q, R, Wr)
-        eng[q].dma_start(out[0], in_[0]).then_inc(T.sem[s], 16)
-        final[s] = 16
-        after(q, (s, 16, dict(know[q]), "dma" + s), R, Wr)
+    def compute(q, R, Wr, steps):
+        def issue():
+            before(q, R, Wr)
+            for step in steps:
+                step(eng[q]).then_inc(T.sem[qsem[q]], 1)
+                cnt[q] += 1
+            final[qsem[q]] = cnt[q]
+            after((qsem[q], cnt[q], dict(know[q]), q), R, Wr)
+        return issue
 
-    def send(dst, name, cols, src, sem):
-        es = topo.engines(core, dst)
-        if topo.chip(core) == topo.chip(dst):
-            es = es[len(es) // 2:]
-        mask = 0
-        for e in es:
-            mask |= 1 << e
-        rid, pid = topo.addr(dst)[0], topo.addr(dst)[1]
-        s = "L%d" % nsem["L"]
-        nsem["L"] += 1
-        before("g", [src], [])
-        o, a = T["t_" + name], T["t_" + src]
-        g.remote_dma(o[:, 0:cols], a[:, 0:cols], T.sem[sem], T.sem[s], pid, rid, mask)
-        final[s] = len(es)
-        after("g", (s, len(es), dict(know["g"]), "rem" + s), [src], [])
+    def emit(R, Wr, *ways):
+        calls.append(([(q, c, c, compute(q, R, Wr, f if isinstance(f, list) else [f])) for q, c, f in ways], R, Wr))
 
-    def arrive(src, name, sem):
-        es = topo.engines(src, core)
-        n = len(es) // 2 if topo.chip(core) == topo.chip(src) else len(es)
-        final[sem] = n
-        last_w[name] = (sem, n, {}, "arr")
+    def dma(q, out, in_, kb):
+        R, Wr = keys_in([in_]) + list(out[2]), [out[1]]
 
-    def B(name, lo=0, hi=None, step=1, key=None):
-        b, at, w = _WHERE[name]
+        def issue():
+            s = "D%d" % nsem["D"]
+            nsem["D"] += 1
+            before(q, R, Wr)
+            eng[q].dma_start(out[0], in_[0]).then_inc(T.sem[s], 16)
+            final[s] = 16
+            after((s, 16, dict(know[q]), "dma" + s), R, Wr)
+        c = 1024 * kb / DMA1 + 0.2
+        calls.append(([(q, c if q == "y" else 0.05, c + DMA0, issue)], R, Wr))
+
+    def engines(src, dst):
+        return [e for e in topo.engines(src, dst) if all(e in topo.engines(src, c) for c in cores if c != src)]
+
+    def send(dst, src_core, name, cols, src, parts):
+        def issue():
+            es = engines(core, dst)
+            mask = 0
+            for e in es:
+                mask |= 1 << e
+            s = "L%d" % nsem["L"]
+            nsem["L"] += 1
+            before("g", parts, [])
+            g.remote_dma(T["t_" + name][:, 0:cols], T["t_" + src][:, 0:cols], T.sem["a_" + name], T.sem[s], topo.addr(dst)[1], topo.addr(dst)[0], mask)
+            final[s] = len(es)
+            after((s, len(es), dict(know["g"]), "rem" + s), parts, [])
+        n = len(engines(src_core, core))
+        final["a_" + name] = n
+        last_w[name] = ("a_" + name, n, {}, "arr")
+        late = REM + REM0 + 256 * cols / REM1
+        calls.append(([("g", REM, late, issue)], parts, ["sent" + name]))
+        calls.append(([("-", 0.0, 0.001, lambda: None)], ["sent" + name], [name]))
+
+    def B(name, lo=0, hi=None, step=1, key=None, more=()):
+        b, at, w, by = _WHERE[name]
         hi = w if hi is None else hi
-        return (T[b][:, at + lo:at + hi:step] if step > 1 else T[b][:, at + lo:at + hi], key or name, ())
+        return (T[b][:, at + lo:at + hi:step] if step > 1 else T[b][:, at + lo:at + hi], key or name, tuple(more), (hi - lo + step - 1) // step, by)
 
-    def P(i, lo, hi, step=1, p0=0, p1=128):
+    def P(i, lo, hi, step=1):
         t = T["p%d" % i]
-        return (t[p0:p1, lo:hi:step] if step > 1 else t[p0:p1, lo:hi], "#%d" % i, ())
+        return (t[:, lo:hi:step] if step > 1 else t[:, lo:hi], "#%d" % i, (), (hi - lo + step - 1) // step, "psum")
 
-    def I(win, off):
-        return (win[0].indirect(off[0]), win[1], (off[1],))
+    PARTS = {"xw": ("xwd",), "gw": ("gw0", "gw1", "gw2", "gw3", "gw4", "gw5"), "fw": ("fwa", "fwb"), "go": ("god",), "ball": ("balld",), "qr": ("qrd",),
+             "cw": ("cwd",), "ra0": ("ra0d",), "ra1": ("ra1d",), "ra2": ("ra2d",), "lfo": ("lfd",), "yl0": ("yld", "yla", "ylb", "ylc")}
+
+    def I(name, off):
+        return (B(name)[0].indirect(off[0]), name, PARTS.get(name, ()) + (off[1],) + off[2], 16 * off[3], "list")
 
     def keys_in(ops):
         return [o[1] for o in ops] + [k for o in ops for k in o[2]]
 
-    def copy(out, in_):
-        emit("v", keys_in([in_]) + list(out[2]), [out[1]], lambda e: e.tensor_copy(out=out[0], in_=in_[0]))
+    def time_v(out, ins, both=False):
+        if out[4] == "list":
+            return 0.05 + out[3] * SC * CY
+        if ins and ins[0][4] == "list":
+            return 0.05 + out[3] * GA * CY
+        n = ins[0][3] if ins else out[3]
+        if both:
+            return max(64, n * (1 if "psum" in (ins[0][4], ins[1][4]) else 2)) * CY
+        return max(64, n * (0.5 if all(o[4] == 2 for o in [out] + ins) else 1)) * CY
+
+    def time_s(in_):
+        return 0.065 + max(64, in_[3] * (GA if in_[4] == "list" else 1)) * CY
+
+    def on_s(out, in_, func, bias=0.0, scale=1.0):
+        x = bias[0] if isinstance(bias, tuple) else bias
+        return ("s", time_s(in_), lambda e: e.activation(out=out[0], in_=in_[0], func=func, bias=x, scale=scale))
+
+    def copy(out, in_, either=False):
+        ways = [("v", time_v(out, [in_]), lambda e: e.tensor_copy(out=out[0], in_=in_[0]))]
+        emit(keys_in([in_]) + list(out[2]), [out[1]], *(ways + [on_s(out, in_, AF.Copy)] * either))
 
     def tt(out, a, b, op):
-        emit("v", keys_in([a, b]) + list(out[2]), [out[1]], lambda e: e.tensor_tensor(out=out[0], in0=a[0], in1=b[0], op=op))
+        emit(keys_in([a, b]) + list(out[2]), [out[1]], ("v", time_v(out, [a, b], True), lambda e: e.tensor_tensor(out=out[0], in0=a[0], in1=b[0], op=op)))
 
-    def ts(out, a, s1, op0, s2=None, op1=None):
+    def ts(out, a, s1, op0, s2=None, op1=None, also=None):
         x1 = s1[0] if isinstance(s1, tuple) else s1
         x2 = s2[0] if isinstance(s2, tuple) else s2
         R = keys_in([x for x in (a, s1, s2) if isinstance(x, tuple)])
         if op1 is None:
-            emit("v", R, [out[1]], lambda e: e.tensor_scalar(out=out[0], in0=a[0], scalar1=x1, scalar2=None, op0=op0))
+            way = ("v", time_v(out, [a]), lambda e: e.tensor_scalar(out=out[0], in0=a[0], scalar1=x1, scalar2=None, op0=op0))
         else:
-            emit("v", R, [out[1]], lambda e: e.tensor_scalar(out=out[0], in0=a[0], scalar1=x1, scalar2=x2, op0=op0, op1=op1))
+            way = ("v", time_v(out, [a]), lambda e: e.tensor_scalar(out=out[0], in0=a[0], scalar1=x1, scalar2=x2, op0=op0, op1=op1))
+        emit(R, [out[1]], *([way] + ([on_s(out, a, *also)] if also else [])))
 
     def scan(out, d0, d1, init, op0, op1):
-        emit("v", keys_in([d0, d1]), [out[1]], lambda e: e.tensor_tensor_scan(out=out[0], data0=d0[0], data1=d1[0], initial=init, op0=op0, op1=op1))
+        x = init[0] if isinstance(init, tuple) else init
+        emit(keys_in([o for o in (d0, d1, init) if isinstance(o, tuple)]), [out[1]],
+             ("v", time_v(out, [d0, d1]), lambda e: e.tensor_tensor_scan(out=out[0], data0=d0[0], data1=d1[0], initial=x, op0=op0, op1=op1)))
+
+    def total(out, in_):
+        emit(keys_in([in_]), [out[1]], ("v", max(64, in_[3]) * CY, lambda e: e.tensor_reduce(out=out[0], in_=in_[0], axis=AxisListType.X, op=OP.add)))
 
     def fill(out, c):
-        emit("v", [], [out[1]], lambda e: e.memset(out[0], c))
+        emit([], [out[1]], ("v", time_v(out, []), lambda e: e.memset(out[0], c)))
 
     def act(out, in_, func, bias=0.0, scale=1.0):
-        emit("s", keys_in([in_]), [out[1]], lambda e: e.activation(out=out[0], in_=in_[0], func=func, bias=bias, scale=scale))
+        emit(keys_in([in_]), [out[1]], on_s(out, in_, func, bias, scale))
 
-    def mm(out, lhsT, rhs, start, stop):
-        emit("t", keys_in([lhsT, rhs]), [out[1]], lambda e: e.matmul(out[0], lhsT[0], rhs[0], start, stop))
+    def signs(out, in_, bias, acc):
+        emit(keys_in([in_, bias]), [out[1], acc[1]],
+             ("s", time_s(in_) + 0.02, lambda e: e.activation(out=out[0], in_=in_[0], func=AF.Sign, bias=bias[0], scale=-1.0, accum_out=acc[0])))
+
+    def mms(group):
+        def step(o, a, b, start, stop):
+            return lambda e: e.matmul(o[0], a[0], b[0], start, stop)
+        R = sorted(set(keys_in([m[1] for m in group] + [m[2] for m in group])))
+        emit(R, [group[0][0][1]], ("t", sum(max(min(64, m[1][3]), m[2][3]) for m in group) * PE, [step(*m) for m in group]))
+
+    def mm(out, *pairs, start=True, stop=True):
+        mms([(out, a, b, start and i == 0, stop and i == len(pairs) - 1) for i, (a, b) in enumerate(pairs)])
 
     def iota(out, pattern, base, cm):
-        fl = out[1] in ("ckey", "ki", "vlo", "dm")
-        if fl:
-            emit("g", [], [out[1]], lambda e: e.iota(out[0], pattern, base, cm, allow_small_or_imprecise_dtypes=True))
+        if out[4] == 2:
+            emit([], [out[1]], ("g", 0.13 + 2 * out[3] * CY, lambda e: e.iota(out[0], pattern, base, cm, allow_small_or_imprecise_dtypes=True)))
         else:
-            emit("g", [], [out[1]], lambda e: e.iota(out[0], pattern, base, cm))
+            emit([], [out[1]], ("g", 0.13 + 2 * out[3] * CY, lambda e: e.iota(out[0], pattern, base, cm)))
+
+    def select(out, in_, op):
+        emit([in_[1]], [out[1]], ("g", 0.17 + 2 * out[3] * CY, lambda e: e.affine_select(out[0], in_[0], [[1, 128]], op, 0.0, 0, -1)))
 
     def wide(name, c):
         return B(name, 15 - c, 143 - c)
 
-    def wrap(bk, lo, sets, n, start=True, stop=True):
-        tot = len(sets) * 16
-        k = 0
-        for wname, rows, r0 in sets:
-            for c in range(16):
-                mm(P(bk, lo, lo + n), wide(wname, c), B(rows, r0 + c, r0 + 16 * n, 16), start and k == 0, stop and k == tot - 1)
-                k += 1
+    def wrap(bk, lo, wname, rows, n, start=True, stop=True, first=0, key=None, more=()):
+        mms([(P(bk, lo + first, lo + n), wide(wname, c), B(rows, 16 * first + c, 16 * n, 16, key=key, more=more), start and c == 0, stop and c == 15)
+             for c in range(16)])
 
-    def lanes(bk, lo, sets):
-        tot = len(sets) * 16
-        k = 0
-        for wname, src, key in sets:
-            for i in range(16):
-                mm(P(bk, lo, lo + CAP), wide(wname, i), B(src, i, 16 * CAP, 16, key=key), k == 0, k == tot - 1)
-                k += 1
-
-    def X(t, key):
-        return (t, key, ())
-
-    dma("y", B("xw", 0, W), X(T.xr[:], "in"))
-    dma("s", B("cxi"), X(T.cx[:], "in"))
-    dma("s", B("qq", 256, 512, key="qr"), X(T.qx[:], "in"))
-    dma("y", B("lfo"), X(T.lf[:], "in"))
-    dma("s", B("tgi"), X(T.tg[:], "in"))
-    dma("y", B("xlo"), X(T.xl[:], "in"))
-    dma("y", B("fdi"), X(T.fd[:], "in"))
-
-    plan = []
-    for d in range(N):
-        hold = [(d, None)]
-        for t in range(RO):
-            u = (d - 1 - t) % N
-            src = hold[0]
-            for h in hold:
-                if topo.chip(cores[h[0]]) == topo.chip(cores[u]):
-                    src = h
-            plan.append((t, src[0], src[1], u))
-            hold.append((u, t))
-
-    def send_disk(t, own):
-        for (tt_, src, held, u) in plan:
-            if tt_ == t and src == rank and (held is None) == own:
-                send(cores[u], "lf%d" % t, M, "lfo" if held is None else "lf%d" % held, "a_lf%d" % t)
-                send(cores[u], "xl%d" % t, M, "xlo" if held is None else "xl%d" % held, "a_xl%d" % t)
-
-    for (t, src, held, u) in plan:
-        if u == rank:
-            arrive(cores[src], "lf%d" % t, "a_lf%d" % t)
-            arrive(cores[src], "xl%d" % t, "a_xl%d" % t)
-    for n, back in (("rd10", 1), ("rd20", 2), ("rd21", 1)):
-        arrive(cores[(rank + back) % N], n, "a_" + n)
-    for t in range(RO):
-        arrive(cores[(rank - 1 - t) % N], "ro%d" % t, "a_ro%d" % t)
-
-    fill(B("ones"), 1.0)
-    emit("g", ["ones"], ["ib"], lambda e: e.affine_select(B("ib")[0], B("ones")[0], [[1, 128]], OP.is_equal, 0.0, 0, -1))
-    iota(B("d1"), [[16, 8], [0, 16]], 15, -1)
-    iota(B("pb"), [[0, 16], [-1, 16]], 0, 1)
-    iota(B("ckey"), [[0, 8], [16, 16]], 0, 0)
-    iota(B("ca"), [[1, 16]], 0, 0)
-    iota(B("kc"), [[0, 16], [1, 16]], 0, 0)
-    iota(B("ki"), [[1, 256]], 0, 0)
-    iota(B("pc"), [[1, 1]], 0, 1)
-    iota(B("vhi"), [[1, 8], [0, 16]], 0, 8)
-    iota(B("vlo"), [[0, 8], [1, 16]], 0, 0)
-    iota(B("dm"), [[1, 6], [0, 16]], 128, 0)
-    for i in range(16):
-        act(B("rr", i, 2048, 16, key="rr"), B("ib"), AF.Copy, scale=-1.0)
-    for kh in range(2):
-        mm(P(5, 128 * kh, 128 * kh + 128), B("qq", 256 + 128 * kh, 384 + 128 * kh, key="qr"), B("ib"), True, True)
-    act(B("qq", 0, 256, key="qt"), P(5, 0, 256), AF.Copy)
-
-    def consts_a():
-        fill(B("xw", W, WD, key="xwd"), 0.0)
-        copy(B("ih"), B("ib"))
-        ts(B("d1s"), B("d1"), 4, OP.arith_shift_right)
-        ts(B("blk"), B("d1s"), 0.0, OP.is_equal)
-        ts(B("sels"), B("blk", 0, 128, 16), 32768.0, OP.mult)
-        ts(B("pbs"), B("pb"), 15, OP.bitwise_and)
-        ts(B("maskb"), B("pbs"), 0.0, OP.is_equal)
-        ts(B("m16"), B("pbs", 0, 16), 0.0, OP.is_equal)
-        copy(B("blk16"), B("blk", 0, 128, 16))
-        copy(B("expl"), B("ca"))
-        ts(B("zz2"), B("kc", 0, 128), 0.0, OP.is_equal, 2.0 * BIG, OP.mult)
-        fill(B("one2"), 1.0)
-        emit("g", ["blk"], ["tri"], lambda e: e.affine_select(B("tri")[0], B("blk")[0], [[1, 128]], OP.is_gt, 0.0, 0, -1))
-        copy(B("cu"), B("cxi"))
-        copy(B("c16"), B("cu"))
-        fill(B("gw", key="gw"), 0.0)
+    def X(t, key, more=()):
+        return (t, key, more)
 
     def col(f):
         return B("m16", f, f + 1)
 
-    def consts_g():
-        ts(B("th"), B("tgi"), 5, OP.arith_shift_right)
-        ts(B("tl"), B("tgi"), 1, OP.arith_shift_right, 15, OP.bitwise_and)
-        ts(B("te"), B("tgi"), 1, OP.bitwise_and)
-        ts(B("vhs"), B("vhi"), 127, OP.bitwise_and)
-        copy(B("gh"), B("th"))
-        copy(B("gl"), B("tl"))
-        copy(B("ge"), B("te"))
-        copy(B("vhb"), B("vhs"))
-        for f, n in ((0, "gh"), (1, "gl"), (2, "vhb"), (3, "vlo"), (4, "ge")):
-            before("y", [n], ["gw"])
-            s = "D%d" % nsem["D"]
-            nsem["D"] += 1
-            g.sync.dma_start(T.t_gw[f:128:16, 0:W], B(n)[0]).then_inc(T.sem[s], 16)
-            final[s] = 16
-            last_w["gw%d" % f] = (s, 16, dict(know["y"]), "dma" + s)
+    def to_row(f, name):
+        dma("y", (T.t_gw[f:128:16, 0:W], "gw%d" % f, ("gw",)), B(name), 32)
 
-    GW = ["gw%d" % f for f in range(6)]
+    def disk_of(t):
+        return cores[(rank + 1 + t) % N]
 
-    def consts_b():
-        ts(B("cv"), col(2), 16.0, OP.mult, col(3), OP.add)
-        ts(B("rv"), B("blk"), B("cv"), OP.mult)
-        ts(B("kadd"), B("ki"), col(6), OP.mult)
-        ts(B("re_"), B("blk"), col(4), OP.mult, -BIG, OP.mult)
-        ts(B("woff"), B("blk"), 65536.0, OP.mult)
-        ts(B("zz"), B("kc"), 0.0, OP.is_equal)
-        ts(B("z1"), B("zz"), 65536.0, OP.mult)
-        ts(B("z0"), B("zz"), -0.5, OP.mult, 0.5, OP.add)
-        scan(B("thrp"), B("z0"), B("z1"), 0.0, OP.mult, OP.add)
-        ts(B("thr"), B("thrp"), -BIG, OP.add)
-        tt(B("z0", 0, 16), B("thrp", 0, 16), B("m16"), OP.mult)
-        emit("v", ["z0"], ["w15"], lambda e: e.tensor_reduce(out=B("w15")[0], in_=B("z0", 0, 16)[0], axis=AxisListType.X, op=OP.add))
-        ts(B("wdiag"), B("blk"), B("w15"), OP.mult, 0.5, OP.mult)
-        fill(B("wb"), 0.0)
-        copy(B("wb", 15, 143, 16), B("blk", 0, 128, 16))
-        ts(B("wb0"), B("wb"), col(0), OP.mult)
-        ts(B("cn"), col(0), 16.0, OP.mult, col(1), OP.add)
-        ts(B("wbn"), B("wb"), B("cn"), OP.mult)
+    def asker_of(t):
+        return cores[(rank - 1 - t) % N]
+
+    dma("y", B("cxi"), X(T.cx[:], "in"), 128)
+    dma("s", B("qr", 0, K), X(T.qx[:], "in"), 64)
+    dma("y", B("xw", 0, W), X(T.xr[:], "in"), 512)
+    dma("s", B("tgi"), X(T.tg[:], "in"), 64)
+    dma("y", B("lfo", 0, M), X(T.lf[:], "in", ("xw",)), 768)
+    dma("y", B("xlo"), X(T.xl[:], "in", ("xw",)), 384)
+    dma("y", B("fdi"), X(T.fd[:], "in", ("xw",)), 512)
+
+    def constants():
+        b16 = B("blk", 0, 128, 16)
+        fill(B("ones"), 1.0)
+        select(B("ib"), B("ones", 0, 128), OP.is_equal)
+        iota(B("d1"), [[16, 8], [0, 16]], 15, -1)
+        iota(B("pb"), [[0, 8], [-1, 16]], 0, 1)
+        iota(B("ckey"), [[0, 8], [16, 16]], 0, 0)
+        iota(B("ca"), [[1, 16]], 0, 0)
+        iota(B("pc"), [[1, 1]], 0, 1)
+        iota(B("kc"), [[0, 16], [1, 16]], 0, 0)
+        iota(B("vhs"), [[16, 8], [0, 16]], 0, 128)
+        iota(B("vlo"), [[0, 8], [1, 16]], 0, 0)
+        for i in range(16):
+            ts(B("rr", i, 2048, 16, key="rr%d" % i), B("ib"), -1.0, OP.mult, also=(AF.Copy, 0.0, -1.0))
+        for name, lo, hi, key in (("gw", 0, WD, "gw"), ("xw", W, WD, "xwd"), ("yl0", M, MD, "yld"), ("ball", K, KD, "balld"), ("qr", K, KD, "qrd"),
+                                  ("ra0", K, KD, "ra0d"), ("ra1", K, KD, "ra1d"), ("ra2", K, KD, "ra2d"), ("wb", 0, 144, "wb"), ("lp01", 0, 128, "lp01"),
+                                  ("lp5", 0, 128, "lp5")):
+            fill(B(name, lo, hi, key=key), 0.0)
+        for name, lo, hi, key in (("fw", W, WD, "fw"), ("lfo", M, MD, "lfd"), ("cw", K, KD, "cwd"), ("ol", 0, 16, "ol")):
+            fill(B(name, lo, hi, key=key), 0)
+        copy(B("ih"), B("ib"))
+        ts(B("d1s"), B("d1"), 4, OP.arith_shift_right)
+        ts(B("pbs"), B("pb"), 15, OP.bitwise_and)
+        ts(B("blk"), B("d1s"), 0.0, OP.is_equal)
+        ts(B("maskb"), B("pbs"), 0.0, OP.is_equal)
+        ts(B("m16"), B("pbs", 0, 16), 0.0, OP.is_equal)
+        ts(B("sels"), b16, 32768.0, OP.mult)
+        copy(B("blk16"), b16)
+        copy(B("blkh"), B("blk"))
+        copy(B("wb", 15, 143, 16), b16)
+        copy(B("expl"), B("ca"))
+        ts(B("zz2"), B("kc", 0, 128), 0.0, OP.is_equal, 2.0 * BIG, OP.mult)
+        select(B("tri"), B("blk"), OP.is_gt)
+        tt(B("imt"), B("ib"), B("tri"), OP.subtract)
+        ts(B("bneg"), B("blk"), -2.0 ** 61, OP.mult, 2.0 ** 61, OP.mult)
+        ts(B("re_"), B("bneg"), col(4), OP.mult, -1.0, OP.mult)
+        ts(B("zz"), B("kc"), 0.0, OP.is_equal, 0.5, OP.mult)
+        ts(B("z0"), B("zz"), 0.5, OP.add)
+        ts(B("top"), B("ones", 0, 1), 2.0 ** 60, OP.mult, 2.0 ** 55, OP.mult)
+        scan(B("thr"), B("z0"), B("ones"), B("top"), OP.mult, OP.mult)
+        tt(B("z1"), B("thr", 0, 16), B("m16"), OP.mult)
+        total(B("w15"), B("z1"))
+        ts(B("pw"), B("w15"), 2.0 ** -50, OP.mult, 2.0 ** -50, OP.mult)
+        ts(B("wdiag"), B("blk"), B("pw"), OP.mult)
         ts(B("pcs"), B("pc"), 15, OP.bitwise_and)
         copy(B("pm"), B("pcs"))
         ts(B("kw"), B("ca"), 16.0, OP.mult, B("pm"), OP.add)
-        ts(B("d257"), B("kw"), 257.0, OP.add)
-        ts(B("d256"), B("kw"), 256.0, OP.add)
-        ts(B("deft"), B("vlo", 0, 96), col(3), OP.mult)
-        ts(B("cc2", 0, 96, key="cc2"), B("dm"), col(2), OP.mult)
-        tt(B("deft"), B("deft"), B("cc2", 0, 96), OP.add)
-
-    def consts_c():
-        ts(B("rk"), B("blk"), col(6), OP.mult)
-        ts(B("wbv"), B("wb"), B("cv"), OP.mult)
-        ts(B("wbk"), B("wb"), col(6), OP.mult)
-        ts(B("rp"), B("blk"), col(4), OP.mult)
+        ts(B("kh5"), B("kw"), 0.5, OP.add)
+        ts(B("dw"), B("kw", 0, 6), float(W), OP.add)
+        ts(B("dw1"), B("kw", 0, 6), float(W + 1), OP.add)
+        ts(B("dm"), B("kw", 0, 6), float(M + 5119), OP.add)
+        tt(B("cn"), col(0), col(1), OP.add)
+        tt(B("cv"), col(2), col(3), OP.add)
+        tt(B("ck"), B("cn"), B("cv"), OP.add)
+        tt(B("cy"), B("cv"), col(5), OP.add)
+        ts(B("cz"), B("cn"), 2.0, OP.mult, col(4), OP.subtract)
+        ts(B("cg"), col(2), FAR, OP.mult, col(4), OP.add)
+        ts(B("ns"), col(0), -0.5, OP.mult, 1.0, OP.add)
+        ts(B("nb"), col(0), 1279.75, OP.mult)
+        ts(B("nw"), col(0), 4.0, OP.mult, col(1), OP.subtract)
+        ts(B("go", K, KD, key="god"), B("ones", 0, 16), B("cg"), OP.mult)
+        for name, c in (("wbn", B("cn")), ("wbv", B("cv")), ("wbh", col(0)), ("wbmh", B("nw")), ("wby", B("cz")), ("wb2", 2.0 ** -8), ("wb2n", -2.0 ** -8)):
+            ts(B(name), B("wb"), c, OP.mult)
+        for name, c, w in (("wbx", 5, 2.0 ** -9), ("wbxn", 5, -2.0 ** -9), ("wbf", 0, FAR)):
+            ts(B(name), B("wb"), col(c), OP.mult, w, OP.mult)
         ts(B("rn"), B("blk"), B("cn"), OP.mult)
-        ts(B("d15w"), B("kw", 0, 6), float(M), OP.add)
-        ts(B("wb2"), B("wb"), 2.0 ** -8, OP.mult)
-        ts(B("wb2n"), B("wb"), -2.0 ** -8, OP.mult)
-        ts(B("wbx"), B("wb"), col(5), OP.mult, 2.0 ** -9, OP.mult)
-        ts(B("wbxn"), B("wb"), col(5), OP.mult, -2.0 ** -9, OP.mult)
+        ts(B("rp"), B("blk"), col(4), OP.mult)
+        ts(B("lp1h"), B("blk"), 0.0, OP.mult)
+        copy(B("lp01", 0, 128, 16), b16)
+        ts(B("lp01", 1, 128, 16), b16, -1.0, OP.mult)
+        copy(B("lp1h", 1, 128, 16), b16)
+        copy(B("lp5", 5, 128, 16), b16)
+        ts(B("ml"), B("ib"), B("ck"), OP.mult)
+        for t in range(RO):
+            tt(B("ld%d" % t), col(4), col(6 + t), OP.add)
+            ts(B("mc%d" % t), B("ib"), B("cy"), OP.mult)
+            ts(B("mc%d" % t, 4, 128, 16), b16, col(6 + t), OP.mult)
 
-    def consts_d():
-        ts(B("d2w"), B("kw", 0, 6), float(W), OP.add)
-        ts(B("d2r"), B("ki", 0, 96), float(W), OP.add)
-        ts(B("sl1"), B("ki", 0, 96), 1024.0, OP.add)
-        ts(B("thrc"), B("thrp", 0, 96), -1024.0, OP.add)
-        copy(B("blkh"), B("blk"))
-        ts(B("blkhn"), B("blk"), -1024.0, OP.mult)
-        copy(B("wbh"), B("wb"))
-        ts(B("wbhn"), B("wb"), -1024.0, OP.mult)
-        for n, f in (("lp0", 0), ("lp1", 1), ("lp4", 4), ("lp5", 5)):
-            fill(B(n), 0.0) if n == "lp5" else ts(B(n), B("blk"), 0.0, OP.mult)
-            copy(B(n, f, 128, 16), B("blk", 0, 128, 16))
-        ts(B("cl"), col(4), -1.0, OP.mult, 1.0, OP.add)
-        tt(B("cc"), B("cl"), col(0), OP.subtract)
-        tt(B("cc"), B("cc"), col(1), OP.subtract)
-        ts(B("maskc"), B("ones", 0, 96), B("cc"), OP.mult)
-        tt(B("cl"), B("cl"), col(5), OP.subtract)
-        ts(B("maskl"), B("ones", 0, 96), B("cl"), OP.mult)
-        copy(B("trih"), B("tri"))
-        ts(B("cy"), B("cn"), 2.0, OP.mult, col(4), OP.add)
-        ts(B("wyt"), B("blk", 0, 128, 16), B("cy"), OP.mult)
+    def tables():
+        ts(B("vht"), B("vhs"), 2047, OP.bitwise_and)
+        copy(B("vhi"), B("vht"))
+        ts(B("tl"), B("tgi"), 1, OP.arith_shift_right)
+        ts(B("te"), B("tgi"), 1, OP.bitwise_and)
+        copy(B("p0"), B("tl"))
+        ts(B("pe"), B("te"), -1.0, OP.mult, 1.0, OP.add)
+        tt(B("p1"), B("tl"), B("p0"), OP.subtract)
+        mms([(P(6, 0, 128), wide("wb", c), B("xw", 128 * c, 128 * c + 128), c == 0, c == 15) for c in range(16)])
+        copy(B("px"), P(6, 0, 128), True)
+        for f, name in enumerate(("p0", "p1", "vhi", "vlo", "pe", "px")):
+            to_row(f, name)
+        copy(B("cu"), B("cxi"))
+        for kh in range(2):
+            mm(P(5, 128 * kh, 128 * kh + 128), (B("qr", 128 * kh, 128 * kh + 128), B("ib")))
+        copy(B("qt"), P(5, 0, 256), True)
 
     def unpack():
-        fill(B("fw", W, WD, key="fw"), 0)
-        copy(B("cw"), B("cxi"))
         ts(B("fw", 0, 1024, key="fwa"), B("fdi"), 2047, OP.bitwise_and)
         ts(B("fw", 1024, 2048, key="fwb"), B("fdi"), 11, OP.arith_shift_right)
 
-    def sums_of_x():
-        for m in range(4):
-            mm(P(6 + m % 2, 0, 512, p1=8), B("blk", 0, 128, 16), B("xw", 512 * m, 512 * m + 512), True, True)
-            emit("s", ["#%d" % (6 + m % 2)], ["sx"], lambda e: e.activation(out=T.t_sx[:, 512 * m:512 * m + 512], in_=P(6 + m % 2, 0, 512, p1=8)[0], func=AF.Copy))
-        before("y", ["sx"], ["gw"])
-        s = "D%d" % nsem["D"]
-        nsem["D"] += 1
-        g.sync.dma_start(T.t_gw[5:128:16, 0:W], T.t_sx[:]).then_inc(T.sem[s], 16)
-        final[s] = 16
-        last_w["gw5"] = (s, 16, dict(know["y"]), "dma" + s)
-
-    def gwin():
-        b = B("gw")
-        return (b[0], "gw", tuple(GW))
-
-    def IG(off):
-        b = B("gw")
-        return (b[0].indirect(off[0]), "gw", tuple(GW) + (off[1],))
-
-    def IX(off):
-        b = B("xw")
-        return (b[0].indirect(off[0]), "xw", ("xwd", off[1]))
-
-    def IF(off):
-        b = B("fw")
-        return (b[0].indirect(off[0]), "fw", ("fwa", "fwb", off[1]))
-
-    def eqs(tile, rows, n, cols, wd, bk, lo, width):
+    def eqs(tile, rows, n, cols, bk, lo, among=None, start=False):
+        width = 16 * n
         for j in range(n):
-            k = "%s%d" % (tile, j)
-            ts(B(tile, width * j + 16 * j, width * j + width, key=k), B(rows, 16 * j, width), B(cols, j, j + 1), OP.is_equal)
-            if j < n - 1:
-                mm(P(bk, lo + 16 * (j + 1), lo + width), B("woff"), B(tile, width * j + 16 * (j + 1), width * j + width, key=k), False, False)
-            mm(P(bk, lo + 16 * j, lo + 16 * j + 16), B("wdiag"), B(tile, width * j + 16 * j, width * j + 16 * j + 16, key=k), False, j == n - 1)
+            e = B(tile, width * j + 16 * j, width * j + width, key="%s%d" % (tile, j))
+            ts(e, B(rows[0], 16 * j, width, key=rows[1], more=rows[2:]), B(cols, j, j + 1), OP.is_equal, 2.0 ** (99 - 15 * j), OP.mult)
+            mm(P(bk, lo + 16 * j, lo + width), (B("wdiag"), e), start=start and j == 0, stop=j == n - 1)
+            if among and j in among:
+                among[j]()
 
-    def choice(t, hooks):
-        def gather(j):
-            o, i_ = B("xc", 512 * j, 512 * j + 512, key="xc%d" % j), IX(B("cu", 32 * j, 32 * j + 32))
-            if j in ON_S:
-                act(o, i_, AF.Copy)
-            else:
-                copy(o, i_)
+    RR = ["rr%d" % i for i in range(16)]
 
-        def differ(j):
-            bk, kh, jj = DB[j % 4], j // 4, j % 4
-            mm(P(bk, 0, 512), B("ib"), B("xc", 512 * j, 512 * j + 512, key="xc%d" % j), True, False)
-            mm(P(bk, 0, 512), B("qq", 128 * kh, 128 * kh + 128, key="qt"), B("rr", 512 * jj, 512 * jj + 512, key="rr"), False, True)
-
-        def dist(j):
-            act(B("ab", 512 * j, 512 * j + 512, key="ab%d" % j), P(DB[j % 4], 0, 512), AF.Abs)
-
-        def keys(kh):
-            kb = 3 + kh
-            mm(P(kb, 0, 128), B("c16", 128 * kh, 128 * kh + 128), B("ih"), True, False)
-            mm(P(kb, 0, 128), B("ones"), B("ckey"), False, False)
-            for i in range(16):
-                o, a, r = P(kb, i, 128, 16), B("ab", 2048 * kh + i, 2048 * kh + 2048, 16), B("sels")
-                emit("t", ["sels"] + ["ab%d" % j for j in range(4 * kh, 4 * kh + 4)], [o[1]], lambda e: e.matmul(o[0], a[0], r[0], False, i == 15))
-
-        does = {"g": gather, "d": differ, "a": dist, "k": keys}
-        for tok in SEQ[t > 0].split():
-            if tok[0] == "h":
-                for h in hooks.get(int(tok[1:]), []):
-                    h()
-            else:
-                does[tok[0]](int(tok[1:]))
+    def choice(t):
+        copy(B("c16"), B("cu"))
         for kh in range(2):
-            scan(B("ks", 128 * kh, 128 * kh + 128, key="ks%d" % kh), B("zz2"), P(3 + kh, 0, 128), 0.0, OP.add, OP.min)
-        emit("v", ["ks0", "ks1"], ["ol"], lambda e: e.tensor_scalar(out=B("ol")[0], in0=B("ks", 15, 256, 16)[0], scalar1=2047, scalar2=None, op0=OP.bitwise_and))
-        tt(B("olm"), I(B("ol"), B("expl")), B("maskb"), OP.mult)
-        for kh in range(2):
-            mm(P(6, 8 * kh, 8 * kh + 8), B("olm", 128 * kh, 128 * kh + 128), B("blk16"), True, True)
-        copy(B("olu"), P(6, 0, 16))
-        copy(B("olf"), P(6, 0, 16))
-        tt(B("go"), IG(B("olu")), B("kadd"), OP.add)
-        mm(P(7, 0, 256), B("rv"), B("go"), True, True)
-        mm(P(5, 0, 256), B("re_"), B("go"), True, False)
+            lo, hi, kb = 128 * kh, 128 * kh + 128, 3 + kh
+            mm(P(kb, 0, 128), (B("c16", lo, hi), B("ih")), (B("ones", 0, 128), B("ckey")), stop=False)
+            for j in range(4 * kh, 4 * kh + 4):
+                xc, d = B("xc", 512 * j, 512 * j + 512, key="xc%d" % j), P(DB[j % len(DB)], 0, 512)
+                copy(xc, I("xw", B("cu", 32 * j, 32 * j + 32)), True)
+                mm(d, (B("ib"), xc), (B("qt", lo, hi), B("rr", 512 * (j % 4), 512 * (j % 4) + 512, key=RR[0], more=RR)))
+                act(B("ab", 512 * j, 512 * j + 512, key="ab%d" % j), d, AF.Abs, bias=128.0 if t else 0.0)
+            mms([(P(kb, i, 128, 16), B("ab", 2048 * kh + i, 2048 * kh + 2048, 16, key="ab%d" % (4 * kh), more=["ab%d" % j for j in range(4 * kh, 4 * kh + 4)]),
+                  B("sels"), False, i == 15) for i in range(16)])
+            e = B("expl", 8 * kh, 8 * kh + 8)
+            scan(B("ks", lo, hi, key="ks%d" % kh), B("zz2"), P(kb, 0, 128), 0.0, OP.add, OP.min)
+            ts(B("ol", 8 * kh, 8 * kh + 8), B("ks", lo + 15, hi, 16, key="ks%d" % kh), 2047, OP.bitwise_and)
+            tt(B("olm", lo, hi, key="olm%d" % kh), I("ol", e), B("maskb"), OP.mult)
+            mm(P(3, 256 + 8 * kh, 264 + 8 * kh), (B("olm", lo, hi, key="olm%d" % kh), B("blk16")))
+            copy(B("ole", lo, hi, key="ole%d" % kh), I("ol", e))
+            mm(P(kb, 128, 256), (B("ole", lo, hi, key="ole%d" % kh), B("ih")))
+            copy(B("orh", lo, hi, key="orh%d" % kh), P(kb, 128, 256))
+        copy(B("cw", 0, K), B("cu"))
 
-    def requests(t, fillers):
-        copy(B("orh"), P(7, 0, 256))
-        eqs("eq", "orh", 16, "olf", None, 5, 0, 256)
-        copy(B("sw", 0, 96), B("deft"))
-        tt(B("cc2", 0, 256), P(5, 0, 256), B("thr"), OP.is_lt)
-        scan(B("cc2", 256, 512, key="cs"), B("one2"), B("cc2", 0, 256), 0.0, OP.mult, OP.add)
-        for f in fillers[0]:
-            f()
-        for c in range(16):
-            l, r = wide("wb0", c), B("cc2", c, 512, 16)
-            emit("t", ["wb0", "cc2", "cs"], ["#6"], lambda e: e.matmul(P(6, 64, 96)[0], l[0], r[0], c == 0, c == 15))
-        tt(B("u1"), P(6, 80, 96), B("d257"), OP.subtract)
-        tt(B("u2"), B("u1"), P(6, 64, 80), OP.mult)
-        tt(B("u3"), B("u2"), B("d256"), OP.add)
-        copy(B("su"), B("u3"))
-        copy(I(B("sw"), B("su")), B("go"))
-        wrap(0, 0, [("wbn", "sw", 0)], 6)
-        mm(P(1, 0, 96), B("rk"), B("sw", 0, 96), True, True)
-        wrap(2, 0, [("wbk", "sw", 0)], 6)
-        wrap(2, 16, [("wbv", "sw", 0)], 6)
-        mm(P(2, 32, 128), B("rn"), B("sw", 0, 96), True, True)
-        mm(P(2, 128, 224), B("rp"), B("sw", 0, 96), True, True)
-        mm(P(7, 0, 96), B("re_"), B("sw", 0, 96), True, False)
-        for f in fillers[1]:
-            f()
-        copy(B("nu"), P(0, 0, 6))
-        copy(B("bf"), I(B("lf%d" % t, 0, M), B("nu")))
-        act(B("s1"), B("bf"), AF.Square, bias=8.0, scale=2.0)
-        act(B("s2"), B("bf"), AF.Square, bias=592.0)
-        copy(B("kru"), P(1, 0, 96))
-        act(B("qe"), (T[_WHERE["qq"][0]][:, _WHERE["qq"][1] + 256:_WHERE["qq"][1] + 512].indirect(B("kru")[0]), "qr", ("kru",)), AF.Copy)
-        ts(B("ci", 0, 96, key="cia"), B("s1"), 32.0 * 2046, OP.add)
-        ts(B("ci", 96, 192, key="cib"), B("s2"), 32.0 * 1337, OP.add)
-        emit("v", ["cia", "cib"], ["cm"], lambda e: e.tensor_scalar(out=B("cm")[0], in0=B("ci")[0], scalar1=5, scalar2=2047, op0=OP.arith_shift_right, op1=OP.bitwise_and))
-        copy(B("cl12"), B("cm"))
+    def requests(t):
+        copy(B("olu"), P(3, 256, 272))
+        copy(B("olf"), P(3, 256, 272))
+        copy(B("go", 0, K), I("gw", B("olu")), True)
+        wrap(0, 0, "wbn", "go", 16)
+        copy(B("nlu"), P(0, 0, 16))
+        send(disk_of(t), asker_of(t), "rq%d" % t, 16, "nlu", ["nlu"])
+        eqs("eq", ("orh", "orh1", "orh0"), 16, "olf", 5, 0, {14: lambda: mm(P(5, 0, 256), (B("re_"), B("go", 0, K)), start=False, stop=False)}, start=True)
+        tt(B("cand"), P(5, 0, 256), B("thr"), OP.is_lt)
+        scan(B("cs"), B("ones"), B("cand"), 0.0, OP.mult, OP.add)
+        a0, acc = 6 - ON_V, ["acc%d" % a for a in range(6)]
+        for a in range(6):
+            junk = B("junk", 256 * a, 256 * a + (256 if a < a0 else 256 - 16 * a0), key="junk%d" % a)
+            if a < a0:
+                signs(junk, B("cs"), B("kh5", a, a + 1), B("acc", a, a + 1, key=acc[a]))
+            else:
+                ts(junk, B("cs", 16 * a0, 256), B("kw", a, a + 1), OP.is_le)
+                total(B("acc", a, a + 1, key=acc[a]), junk)
+        ts(B("klu", a0, 6, key="klb"), B("acc", a0, 6, key=acc[5], more=acc[a0:]), 16.0 * a0, OP.add)
+        ts(B("klu", 0, a0), B("acc", 0, a0, key=acc[0], more=acc[:a0]), 0.5, OP.mult, 128.0, OP.add)
+        copy(B("sb"), I("lfo", B("rq%d" % t)))
+        send(asker_of(t), disk_of(t), "rb%d" % t, K, "sb", ["sb"])
+        copy(B("sa"), I("xlo", B("rq%d" % t)), True)
+        send(asker_of(t), disk_of(t), "ra%d" % t, K, "sa", ["sa"])
+        kl = B("klu", more=["klb"])
+        copy(B("csu"), I("cw", kl))
+        ts(B("qc"), I("qr", kl), -128.0 if t else 0.0, OP.add, also=(AF.Identity, -128.0 if t else 0.0))
+        copy(B("sw"), I("go", kl), True)
+        wrap(1, 0, "wbv", "sw", 6)
+        tt(B("u1"), P(1, 0, 6), B("dw"), OP.min)
+        copy(B("osu"), B("u1"))
+        for i in range(16):
+            copy(B("qe", i, 1536, 16, key="qe%d" % i), B("qc"), True)
+        copy(B("ball", 0, K), B("rb%d" % t))
+        act(B("s1"), I("ball", kl), AF.Square, bias=8.0, scale=2.0)
+        act(B("s2"), I("ball", kl), AF.Square, bias=592.0)
+        copy(B("bf"), I("ball", kl), True)
+        copy(B("at"), I("ra%d" % t, kl), True)
+        for c, (s, add) in enumerate((("s1", 32.0 * 2046), ("s2", 32.0 * 1337))):
+            lo, hi = 96 * c, 96 * c + 96
+            ts(B("ci", lo, hi, key="ci%d" % c), B(s), add, OP.add)
+            ts(B("cm", lo, hi, key="cm%d" % c), B("ci", lo, hi, key="ci%d" % c), 5, OP.arith_shift_right, 2047, OP.bitwise_and)
+            copy(B("cl12", lo, hi, key="cl%d" % c), B("cm", lo, hi, key="cm%d" % c))
 
-    def later_lists(t):
-        copy(B("klu"), P(2, 0, 6))
-        copy(B("osu"), P(2, 16, 22))
-        copy(B("nrh"), P(2, 32, 128))
-        copy(B("pr"), P(2, 128, 224))
-        copy(B("nl"), P(0, 0, 6))
-        copy(B("csu"), I(B("cw"), B("klu")))
+    def disk_writes(t):
+        for h in range(3):
+            copy(B("gs", 512 * h, 512 * h + 512, key="gs%d" % h), I("gw", B("csu", 32 * h, 32 * h + 32)), True)
+        wrap(6, 0, "wbn", "gs", 96, key="gs0", more=("gs1", "gs2"))
+        copy(B("db", 6, DW, key="dbb"), P(6, 0, 96))
+        mm(P(7, 0, 96), (B("rn"), B("sw")))
+        wrap(7, 96, "wbn", "sw", 6)
+        copy(B("nrh"), P(7, 0, 96))
+        copy(B("nl"), P(7, 96, 102), True)
+        mm(P(7, 128, 224), (B("re_"), B("sw")), stop=False)
+        ts(B("nh"), B("nrh"), B("ns"), OP.mult, B("nb"), OP.add)
+        wrap(0, 128, "wbmh", "nh", 6, stop=False)
+        eqs("eqn", ("nrh", "nrh"), 6, "nl", 7, 128)
+        tt(B("lsn"), P(7, 128, 224), B("thr", 0, 96), OP.is_ge)
+        wrap(0, 128, "wbf", "lsn", 6, start=False)
+        tt(B("u2"), P(0, 128, 134), B("dm"), OP.min)
+        ts(B("db", 0, 6, key="dba"), B("u2"), -5119.0, OP.add)
+        send(disk_of(t), asker_of(t), "rd%d" % t, DW, "db", ["dba", "dbb"])
 
-    def dedupe_n(t):
-        eqs("eqn", "nrh", 6, "nl", None, 7, 0, 96)
+    def apply(dst, t):
+        copy(I(dst, B("rd%d" % t, 0, 6)), B("rd%d" % t, 6, DW))
 
-    def dedupe_n2(t):
-        tt(B("mfl"), P(7, 0, 96), B("thr", 0, 96), OP.is_lt)
-        wrap(7, 128, [("wb0", "mfl", 0)], 6)
-        copy(B("nli"), B("nl"))
-        ts(B("nb"), B("nli"), 1, OP.bitwise_and)
-        ts(B("mn1"), B("nb"), -2.0, OP.mult, 1.0, OP.add)
-        tt(B("mn2"), B("mn1"), B("nl"), OP.add)
-        tt(B("mn3"), B("mn2"), B("d15w"), OP.subtract)
-        tt(B("mn4"), B("mn3"), P(7, 128, 134), OP.mult)
-        tt(B("mn5"), B("mn4"), B("d15w"), OP.add)
-        copy(B("db%d" % t, 0, 6, key="dba%d" % t), B("mn5"))
+    QE = ["qe%d" % i for i in range(16)]
 
-    def long_names(t):
-        act(B("gs"), IG(B("csu")), AF.Copy)
-        lanes(6, 400, [("wbn", "gs", "gs")])
-
-    def send_delta(t):
-        copy(B("db%d" % t, 6, DW, key="dbb%d" % t), P(6, 400, 496))
-        last_w["db%d" % t] = last_w["dbb%d" % t]
-        wait("g", last_w["dba%d" % t])
-        for k, (back, name) in enumerate({0: ((1, "rd10"), (2, "rd20")), 1: ((1, "rd21"),), 2: ()}[t]):
-            send(cores[(rank - back) % N], name, DW, "db%d" % t, "a_" + name)
-        send(cores[(rank + 1 + t) % N], "ro%d" % t, DW, "db%d" % t, "a_ro%d" % t)
-
-    def apply(dst, src):
-        copy(I(B(dst), B(src, 0, 6)), B(src, 6, DW))
-
-    def translate(t, fillers):
-        tt(B("m1"), IX(B("cl12", 0, 96)), B("qe"), OP.max)
-        act(B("g1"), IG(B("cl12", 0, 96)), AF.Copy)
-        lanes(4, 0, [("wbn", "g1", "g1")])
-        def part(wname, src, lo, hi, key, start=False, stop=False):
-            for i in range(16):
-                mm(P(3, lo, hi), wide(wname, i), B(src, 16 * lo + i, 16 * hi, 16, key=key), start and i == 0, stop and i == 15)
-        part("wb2n", "m1", 0, 96, "m1", start=True)
-        part("wbx", "g1", 0, 96, "g1")
-        H = HALF
-        act(B("at"), I(B("xl%d" % t), B("nu")), AF.Copy)
-        tt(B("m2", 0, 16 * H, key="m2a"), IX(B("cl12", 96, 96 + H)), B("qe", 0, 16 * H), OP.max)
-        act(B("g2", 0, 16 * H, key="g2a"), IG(B("cl12", 96, 96 + H)), AF.Copy)
-        act(B("g2", 16 * H, 1536, key="g2b"), IG(B("cl12", 96 + H, 192)), AF.Copy)
-        tt(B("m2", 16 * H, 1536, key="m2b"), IX(B("cl12", 96 + H, 192)), B("qe", 16 * H, 1536), OP.max)
-        part("wb2", "m2", 0, H, "m2a")
-        part("wbxn", "g2", 0, H, "g2a")
-        for lo, hi, key in ((0, H, "g2a"), (H, 96, "g2b")):
-            for i in range(16):
-                mm(P(4, 96 + lo, 96 + hi), wide("wbn", i), B("g2", 16 * lo + i, 16 * hi, 16, key=key), i == 0, i == 15)
-        part("wbxn", "g2", H, 96, "g2b")
-        part("wb2", "m2", H, 96, "m2b", stop=True)
-        long_names(t)
-        copy(B("bb", 0, 96, key="bba"), B("bf"))
-        copy(B("bb", 96, 192, key="bbb"), B("bf"))
-        copy(B("c1f"), B("cm", 0, 96))
-        tt(B("dcf"), B("cm", 96, 192), B("cm", 0, 96), OP.subtract)
-        copy((B("xw")[0].indirect(B("osu")[0]), "xw", ("xwd", "osu")), B("at"))
-        copy(B("bi"), B("bf"))
-        ts(B("bhi"), B("bi"), 4, OP.arith_shift_right)
-        ts(B("blo"), B("bi"), 15, OP.bitwise_and)
-        for f in fillers[2]:
-            f()
-        emit("v", ["#4", "bba", "bbb"], ["e12"], lambda e: e.tensor_tensor(out=B("e12")[0], in0=P(4, 0, 192)[0], in1=B("bb")[0], op=OP.is_equal))
-        tt(B("wf"), P(3, 0, 96), B("e12", 96, 192), OP.max)
-        tt(B("chf"), B("wf"), B("e12", 0, 96), OP.is_gt)
-        tt(B("sx1"), B("chf"), B("dcf"), OP.mult)
-        tt(B("sf"), B("sx1"), B("c1f"), OP.add)
-        copy((B("fw")[0].indirect(B("osu")[0]), "fw", ("fwa", "fwb", "osu")), B("sf"))
+    def translate(t):
+        def piece(c, lo, hi, key):
+            cl = B("cl12", 96 * c + lo, 96 * c + hi, key="cl%d" % c)
+            tt(B("m%d" % (c + 1), 16 * lo, 16 * hi, key="m" + key), I("xw", cl), B("qe", 16 * lo, 16 * hi, key="qe0", more=QE), OP.max)
+            copy(B("g%d" % (c + 1), 16 * lo, 16 * hi, key="g" + key), I("gw", cl), True)
+        piece(0, 0, 48, "1a")
+        piece(0, 48, 96, "1b")
+        piece(1, 0, HALF, "2a")
+        piece(1, HALF, 96, "2b")
+        wrap(4, 0, "wbn", "g1", 96, key="g1a", more=("g1b",))
+        tt(B("e1"), P(4, 0, 96), B("bf"), OP.is_equal)
+        wrap(3, 0, "wbx", "g1", 96, stop=False, key="g1a", more=("g1b",))
+        wrap(3, 0, "wb2n", "m1", 96, start=False, stop=False, key="m1a", more=("m1b",))
+        wrap(5, 0, "wbn", "g2", HALF, key="g2a")
+        wrap(3, 0, "wbxn", "g2", HALF, start=False, stop=False, key="g2a")
+        wrap(3, 0, "wb2", "m2", HALF, start=False, stop=False, key="m2a")
+        wrap(5, 0, "wbn", "g2", 96, first=HALF, key="g2b")
+        wrap(3, 0, "wbxn", "g2", 96, start=False, stop=False, first=HALF, key="g2b")
+        wrap(3, 0, "wb2", "m2", 96, start=False, first=HALF, key="m2b")
+        copy(I("xw", B("osu")), B("at"))
+        copy(B("xo"), I("xw", B("olu")), True)
+        tt(B("dcf"), B("cm", 96, 192, key="cm1"), B("cm", 0, 96, key="cm0"), OP.subtract)
+        tt(B("e2"), P(5, 0, 96), B("bf"), OP.is_equal)
+        tt(B("wf"), P(3, 0, 96), B("e2"), OP.max)
+        tt(P(4, 128, 224), B("wf"), B("e1"), OP.is_gt)
+        tt(P(4, 256, 352), P(4, 128, 224), B("dcf"), OP.mult)
+        tt(B("sf"), P(4, 256, 352), B("cm", 0, 96, key="cm0"), OP.add)
+        copy(I("fw", B("osu")), B("sf"))
 
     def moves(t):
         last = t == RO - 1
-        copy(B("ycf") if last else B("cu"), IF(B("olu")))
-        act(B("xo"), IX(B("olu")), AF.Identity, bias=-0.5)
-        halves = ((256, 512, "qr"),) if last else ((0, 256, "qt"), (256, 512, "qr"))
-        for lo, hi, key in halves:
-            if key == "qt":
-                for kh in range(2):
-                    o = P(5, 128 * kh, 128 * kh + 128)
-                    mm(o, B("xo", 128 * kh, 128 * kh + 128), B("ib"), True, False)
-                    mm(o, B("qq", 256 + 128 * kh, 384 + 128 * kh, key="qr"), B("ib"), False, True)
-            else:
-                mm(P(5, 256, 512), B("ib"), B("xo"), True, False)
-                mm(P(5, 256, 512), B("ib"), B("qq", 256, 512, key="qr"), False, True)
-        for lo, hi, key in halves:
-            act(B("zf", lo, hi, key="zf" + key), P(5, lo, hi), AF.Identity, scale=0.5, bias=MAGIC)
-            act(B("qq", lo, hi, key=key), B("zf", lo, hi, key="zf" + key), AF.Identity, bias=-MAGIC)
+        copy(B("ycf") if last else B("cu"), I("fw", B("olu")))
+        bias = 63.75 if t else 127.75
         if not last:
-            copy(B("c16"), B("cu"))
+            for kh in range(2):
+                lo, hi = 128 * kh, 128 * kh + 128
+                mm(P(2, lo, hi), (B("xo", lo, hi), B("ib")), (B("qr", lo, hi), B("ib")))
+            ts(B("qt"), P(2, 0, 256), 0.5, OP.mult, bias, OP.add, also=(AF.Identity, bias, 0.5))
+        mm(P(1, 256, 512), (B("ib"), B("xo")), (B("ib"), B("qr", 0, K)))
+        ts(B("qr", 0, K), P(1, 256, 512), 0.5, OP.mult, bias, OP.add, also=(AF.Identity, bias, 0.5))
+        if last:
+            ts(B("yqb"), B("qr", 0, K), -128.0, OP.add, also=(AF.Identity, -128.0))
 
     def claims(t):
-        def c0():
-            if t < RO - 1:
-                copy(B("cw"), B("cu"))
-            tt(B("tmx"), B("e12", 0, 96), B("e12", 96, 192), OP.max)
-            tt(B("nr"), B("pr"), B("tmx"), OP.is_gt)
-            mm(P(6, 128, 224), B("trih"), B("nr"), True, True)
-            tt(B("sp"), B("sf"), B("sl1"), OP.subtract)
+        mm(P(6, 256, 352), (B("ml"), B("sw")), (B("lp5"), B("at")))
+        ts(B("gl"), P(6, 256, 352), B("ld%d" % t), OP.add, also=(AF.Identity, B("ld%d" % t)))
+        copy(I("gw", B("osu")), B("gl"))
+        mm(P(5, 128, 224), (B("rp"), B("sw")), (B("ib"), B("e1")), (B("ib"), B("e2")))
+        ts(B("nr"), P(5, 128, 224), 0.0, OP.is_equal, also=(AF.Relu, 1.0, -1.0))
+        mm(P(5, 256, 352), (B("imt"), B("nr")))
+        ts(B("f1"), P(5, 256, 352), 0.0, OP.max, also=(AF.Relu,))
+        tt(B("fv"), B("f1"), B("sf"), OP.mult)
+        mm(P(5, 384, 480), (B("blkh"), B("fv")), (B("blk"), B("f1")))
+        tt(B("fb"), B("f1"), B("bf"), OP.mult)
+        copy(B("fb0"), B("fb"))
+        copy(B("vrh"), P(5, 384, 480))
+        wrap(5, 0, "wbh", "vrh", 6)
+        mm(P(7, 384, 480), (B("re_"), B("ones", 0, 96)), (B("bneg"), B("f1")), stop=False)
+        copy(B("vl"), P(5, 0, 6), True)
+        eqs("eqc", ("vrh", "vrh"), 6, "vl", 7, 384)
+        tt(B("lsc"), P(7, 384, 480), B("thr", 0, 96), OP.is_ge)
+        wrap(5, 16, "wbf", "lsc", 6)
+        tt(B("u4"), P(5, 16, 22), B("vl"), OP.max)
+        tt(B("u3"), B("u4"), B("dw1"), OP.min)
+        ts(B("vu"), B("u3"), -1.0, OP.add)
+        copy(B("old"), I("gw", B("vu")), True)
+        mm(P(7, 0, 96), (B("lp01"), B("fb0")), (B("lp1h"), B("fb")), (B("mc%d" % t), B("old")))
+        copy(B("gn"), P(7, 0, 96), True)
+        copy(I("gw", B("vu")), B("gn"))
 
-        def c1():
-            tt(B("f1"), B("nr"), P(6, 128, 224), OP.is_gt)
-            tt(B("fv"), B("f1"), B("sp"), OP.mult)
-            wrap(6, 256, [("wbh", "fv", 0), ("wbhn", "f1", 0)], 6)
-            mm(P(6, 288, 384), B("blkh"), B("fv"), True, False)
-            mm(P(6, 288, 384), B("blkhn"), B("f1"), False, True)
-            mm(P(7, 256, 352), B("blkhn"), B("f1"), True, False)
-            tt(B("fbh"), B("f1"), B("bhi"), OP.mult)
-            tt(B("fbl"), B("f1"), B("blo"), OP.mult)
-
-        def c2():
-            tt(B("vl"), P(6, 256, 262), B("d2w"), OP.add)
-            tt(B("vrh"), P(6, 288, 384), B("d2r"), OP.add)
-            eqs("eqc", "vrh", 6, "vl", None, 7, 256, 96)
-
-        def c3():
-            tt(B("cfl"), P(7, 256, 352), B("thrc"), OP.is_lt)
-            wrap(6, 272, [("wb0", "cfl", 0)], 6)
-            mm(P(7, 384, 480), B("lp0"), B("fbh"), True, False)
-            mm(P(7, 384, 480), B("lp1"), B("fbl"), False, False)
-            mm(P(7, 384, 480), B("lp4"), B("f1"), False, True)
-            mm(P(7, 128, 224), B("lp5"), B("at"), True, True)
-            tt(B("vt1"), B("vl"), B("d2w"), OP.subtract)
-
-        def c4():
-            tt(B("vt2"), B("vt1"), P(6, 272, 278), OP.mult)
-            tt(B("vt3"), B("vt2"), B("d2w"), OP.add)
-            copy(B("vu"), B("vt3"))
-            tt(B("gvm"), IG(B("vu")), B("maskc"), OP.mult)
-            tt(B("gn"), B("gvm"), P(7, 384, 480), OP.add)
-            copy((B("gw")[0].indirect(B("vu")[0]), "gw", tuple(GW) + ("vu",)), B("gn"))
-
-        def c5():
-            tt(B("glm"), IG(B("osu")), B("maskl"), OP.mult)
-            tt(B("gl2"), B("glm"), P(7, 128, 224), OP.add)
-            copy((B("gw")[0].indirect(B("osu")[0]), "gw", tuple(GW) + ("osu",)), B("gl2"))
-        return [c0, c1, c2, c3, c4, c5]
-
-    consts_a()
-    send_disk(0, True)
-    hooks = {1: [consts_g], 2: [consts_b, sums_of_x], 3: [unpack]}
+    constants()
+    tables()
     for t in range(RO):
-        choice(t, hooks)
+        choice(t)
+        requests(t)
         if t == 0:
-            send_disk(1, True)
-            send_disk(1, False)
-            send_disk(2, True)
-            fillers = [[consts_c], [], [consts_d]]
-        elif t == 1:
-            fillers = [[], [lambda: apply("lf1", "rd10")], [lambda: copy(B("yl0", 0, M), B("lfo"))]]
-        else:
-            fillers = [[lambda: apply("lf2", "rd20")], [lambda: apply("lf2", "rd21")], [lambda: apply("yl0", "ro0"), lambda: apply("yl0", "ro1")]]
-        requests(t, fillers)
-        later_lists(t)
-        dedupe_n(t)
-        dedupe_n2(t)
-        translate(t, fillers)
+            unpack()
+        if t == RO - 1:
+            for h in range(3):
+                copy(B("yl0", 512 * h, 512 * h + 512, key="yl" + "abc"[h]), B("lfo", 512 * h, 512 * h + 512))
+        disk_writes(t)
+        translate(t)
         moves(t)
-        cl = claims(t)
-        if t < RO - 1:
-            tp = [t]
-            hooks = {0: [lambda: send_delta(tp[0]), cl[0]], 1: [cl[1]], 2: [cl[2]], 3: [cl[3]], 4: [cl[4]], 5: [cl[5]]}
-            if t == 0:
-                hooks[0].append(lambda: send_disk(2, False))
-        else:
-            send_delta(t)
-            dma("y", X(T.yc[:], "yc"), B("ycf"))
-            dma("y", X(T.yq[:], "yq"), B("qq", 256, 512, key="qr"))
-            for c in cl[:5]:
-                c()
-            apply("yl0", "ro2")
-            dma("y", X(T.yl[:], "yl"), B("yl0", 0, M))
-            cl[5]()
-            for m in range(4):
-                emit("t", ["wyt", "gw"], ["#%d" % m], lambda e: e.matmul(P(m, 0, 512, p1=8)[0], B("wyt")[0], B("gw", 512 * m, 512 * m + 512)[0], True, True))
-                o = T.t_ytf[0:8, 512 * m:512 * m + 512]
-                if m % 2:
-                    emit("s", ["#%d" % m], ["ytf%d" % m], lambda e: e.activation(out=o, in_=P(m, 0, 512, p1=8)[0], func=AF.Copy))
-                else:
-                    emit("v", ["#%d" % m], ["ytf%d" % m], lambda e: e.tensor_copy(out=o, in_=P(m, 0, 512, p1=8)[0]))
-            dma("y", X(T.yt[:], "yt"), (T.t_ytf[0:8, :], "ytf0", ("ytf1", "ytf2", "ytf3")))
+        claims(t)
+        apply("lfo" if t < RO - 1 else "yl0", t)
+    dma("y", X(T.yl[:], "yl"), B("yl0", 0, M, more=PARTS["yl0"]), 768)
+    dma("y", X(T.yc[:], "yc"), B("ycf"), 128)
+    dma("y", X(T.yq[:], "yq"), B("yqb"), 64)
+    mms([(P(0, 0, 128), wide("wby", c), B("gw", 128 * c, 128 * c + 128), c == 0, c == 15) for c in range(16)])
+    ts(B("ytf"), P(0, 0, 128), 1.0, OP.add, also=(AF.Identity, 1.0))
+    dma("y", X(T.yt[:], "yt"), B("ytf"), 64)
+    if not ORDER:
+        ORDER.extend(in_order(calls))
+    for n, way in ORDER:
+        calls[n][0][way][3]()
     for s in sorted(final):
         if know["g"].get(s, 0) < final[s]:
             g.wait_ge(T.sem[s], final[s])

from concourse.bass import DstId, RemoteDMATransfer
from concourse.mybir import AluOpType as OP, AxisListType, ActivationFunctionType as AF

N, W, M, K, CAP, RO = 6, 2048, 1536, 256, 96, 3
KD = K + 16
WD, MD = W + CAP, M + CAP
BIG = 16777216.0
FAR = 8192.0
DW = 6 + CAP
DB = (0, 1, 2)
HALF = 64
ON_V = 2
CY, PE, GA, SC, OWN, HOP, DMA0, DMA1, REM, REM0, REM1 = 0.9e-3, 0.46e-3, 1.56, 3.8, 0.06, 0.1, 1.6, 250e3, 0.4, 1.7, 60e3
KEEP, ROUNDS = 0.3, 6
ORDER = []

SCRATCH = {}
_d = {
    "float32": dict(m16=16, pm=1, pw=1, w15=1, cn=1, cv=1, cy=1, cz=1, cg=1, ck=1, ns=1, nb=1, nw=1, top=1, ld0=1, ld1=1, ld2=1, thr=256, z0=256, z1=16, zz=256,
                    kw=16, kh5=16, dw=6, dw1=6, dm=6, olf=16, acc=8, ball=KD, bf=96, s1=96, s2=96, dcf=96, sf=96, nl=6, vl=6, u1=6, u2=6, u3=6, u4=6,
                    yl0=MD, ycf=256, ytf=128, zz2=128),
    "bfloat16": dict(ib=128, imt=128, rr=2048, ones=256, blk=128, sels=8, ckey=128, vlo=128, vhi=128, wdiag=128, tri=128, re_=128,
                     rn=128, rp=128, bneg=128, lp01=128, lp5=128, ml=128, mc0=128, mc1=128, mc2=128,
                     wb=144, wbn=144, wbv=144, wbf=144, wby=144, wbx=144, wbxn=144, wb2=144, wb2n=144, xw=WD, gw=WD, xlo=M, xc=4096, ab=4096,
                     qt=256, qr=KD, xo=256, go=KD, eq=4096, cand=256, cs=256, junk=1536, sw=96, at=96, qc=96, qe=1536, g1=1536, g2=1536, gs=1536,
                     m1=1536, m2=1536, wf=96, e1=96, e2=96, eqn=576, lsn=96, eqc=576, lsc=96, nr=96, f1=96, fb0=96, old=96, gn=96, gl=96,
                     p0=128, p1=128, pe=128, px=128, sa=256, ra0=KD, ra1=KD, ra2=KD, yqb=256),
    "float16": dict(ih=128, maskb=128, blk16=8, blkh=128, lp1h=128, wbh=144, wbmh=144, c16=256, olm=256, ole=256, orh=256, nrh=96, nh=96, fv=96, fb=96, vrh=96),
    "int32": dict(d1=128, pb=128, kc=256, ca=16, pc=1, d1s=128, pbs=128, pcs=1, vhs=128, vht=128, cxi=256, cw=KD, fdi=1024, fw=WD, tgi=128, tl=128, te=128,
                  lfo=MD, ks=256, ol=16, ci=192, cm=192),
    "uint16": dict(expl=16, cu=256, olu=16, nlu=16, klu=6, osu=6, csu=96, cl12=192, vu=6, sb=256, db=DW,
                   rq0=16, rq1=16, rq2=16, rb0=256, rb1=256, rb2=256, rd0=DW, rd1=DW, rd2=DW),
}
_WHERE = {}
_SOLO = ("xw", "gw", "fw", "xlo", "lfo", "yl0", "xc", "ab", "cw", "fdi", "cxi", "tgi", "ol", "ytf", "ycf", "cl12", "qr", "go", "ball", "nlu", "sb", "sa", "db",
         "rq0", "rq1", "rq2", "rb0", "rb1", "rb2", "ra0", "ra1", "ra2", "rd0", "rd1", "rd2")
for _dt in _d:
    _small, _at, _by = "pool_" + _dt, 0, 4 if _dt.endswith("32") else 2
    for _n in _d[_dt]:
        _c = _d[_dt][_n]
        if _n in _SOLO:
            SCRATCH["t_" + _n] = ("sbuf", [128, _c], _dt)
            _WHERE[_n] = ("t_" + _n, 0, _c, _by)
        else:
            _WHERE[_n] = (_small, _at, _c, _by)
            _at += (_c + 15) // 16 * 16
    SCRATCH[_small] = ("sbuf", [128, _at], _dt)
for _i in range(8):
    SCRATCH["p%d" % _i] = ("psum", [128, 512], "float32")

SEMAPHORES = (["sv", "ss", "st", "sg"] + ["D%d" % i for i in range(24)] + ["L%d" % i for i in range(12)]
              + ["a_%s%d" % (n, i) for n in ("rq", "rb", "ra", "rd") for i in range(RO)])


def in_order(calls):
    pred, writer, readers = [], {}, {}
    for n, (ways, R, Wr) in enumerate(calls):
        p = set(writer[k] for k in R + Wr if k in writer)
        for k in Wr:
            p.update(readers.get(k, ()))
        for k in R:
            readers.setdefault(k, []).append(n)
        for k in Wr:
            writer[k], readers[k] = n, []
        p.discard(n)
        pred.append(sorted(p))
    succ = [[] for _ in calls]
    for n in range(len(calls)):
        for p in pred[n]:
            succ[p].append(n)

    def place(order, needs, back):
        busy, placed = {}, {}
        for n in order:
            best = None
            for w in calls[n][0]:
                lead = w[2] - w[1] if back else 0.0
                at = lead
                for p in needs[n]:
                    end, pw = placed[p]
                    at = max(at, end + lead + (HOP if pw[0] != w[0] else 0.001 if w[0] == "t" else OWN))
                for a, b in busy.get(w[0], ()):
                    if at + w[1] <= a:
                        break
                    at = max(at, b)
                end = at - lead + w[2]
                if best is None or end + (KEEP if w[0] == "v" else 0.0) < best[0]:
                    best = (end + (KEEP if w[0] == "v" else 0.0), end, at, w)
            placed[n] = (best[1], best[3])
            if best[3][1] > 0:
                busy.setdefault(best[3][0], []).append((best[2], best[2] + best[3][1]))
                busy[best[3][0]].sort()
        return placed

    every = range(len(calls))
    order, best = list(every), None
    for _ in range(ROUNDS):
        back = place(order[::-1], succ, True)
        ahead = place(sorted(every, key=lambda i: (-back[i][0], i)), pred, False)
        order = sorted(every, key=lambda i: (ahead[i][0], i))
        if best is None or ahead[order[-1]][0] < best[0]:
            best = (ahead[order[-1]][0], ahead)
    ahead = best[1]
    return [(n, calls[n][0].index(ahead[n][1])) for n in sorted(every, key=lambda i: (ahead[i][0] - ahead[i][1][2], i))]


def rank_program(g, core, T, topo):
    rank = T.rank_of(core)
    if rank is None:
        return
    cores = list(T.cores)
    eng = {"v": g.vector, "s": g.scalar, "t": g.tensor, "g": g, "y": g.sync}
    qsem = {"v": "sv", "s": "ss", "t": "st", "g": "sg"}
    cnt = {"v": 0, "s": 0, "t": 0, "g": 0}
    know = {q: {} for q in eng}
    calls, last_w, readers, bank, final, nsem = [], {}, {}, {}, {}, {"D": 0, "L": 0}

    def wait(q, ev):
        sem, val, snap = ev[0], ev[1], ev[2]
        if know[q].get(sem, 0) >= val:
            return
        eng[q].wait_ge(T.sem[sem], val)
        know[q][sem] = val
        for s in snap:
            if know[q].get(s, 0) < snap[s]:
                know[q][s] = snap[s]

    def before(q, R, Wr):
        for k in R + Wr:
            if k in last_w and not (last_w[k][3] == q and q == "t"):
                wait(q, last_w[k])
        for k in Wr:
            for rq in readers.get(k, {}):
                wait(q, readers[k][rq])
        for k in R:
            if k[0] == "#":
                for rq in readers.get(k, {}):
                    if rq != q:
                        wait(q, readers[k][rq])

    def after(ev, R, Wr):
        for k in R:
            readers.setdefault(k, {})[ev[3]] = ev
        for k in Wr:
            last_w[k] = ev
            readers[k] = {}

    def compute(q, R, Wr, steps):
        def issue():
            before(q, R, Wr)
            for step in steps:
                step(eng[q]).then_inc(T.sem[qsem[q]], 1)
                cnt[q] += 1
            final[qsem[q]] = cnt[q]
            after((qsem[q], cnt[q], dict(know[q]), q), R, Wr)
        return issue

    def emit(R, Wr, *ways):
        calls.append(([(q, c, c, compute(q, R, Wr, f if isinstance(f, list) else [f])) for q, c, f in ways], R, Wr))

    def dma(q, out, in_, kb):
        R, Wr = keys_in([in_]) + list(out[2]), [out[1]]

        def issue():
            s = "D%d" % nsem["D"]
            nsem["D"] += 1
            before(q, R, Wr)
            eng[q].dma_start(out[0], in_[0]).then_inc(T.sem[s], 16)
            final[s] = 16
            after((s, 16, dict(know[q]), "dma" + s), R, Wr)
        c = 1024 * kb / DMA1 + 0.2
        calls.append(([(q, c if q == "y" else 0.05, c + DMA0, issue)], R, Wr))

    def engines(src, dst):
        return [e for e in topo.engines(src, dst) if all(e in topo.engines(src, c) for c in cores if c != src)]

    def send(dst, src_core, name, cols, src, parts):
        def issue():
            es = engines(core, dst)
            mask = 0
            for e in es:
                mask |= 1 << e
            s = "L%d" % nsem["L"]
            nsem["L"] += 1
            before("g", parts, [])
            g.remote_dma(T["t_" + name][:, 0:cols], T["t_" + src][:, 0:cols], T.sem["a_" + name], T.sem[s], topo.addr(dst)[1], topo.addr(dst)[0], mask)
            final[s] = len(es)
            after((s, len(es), dict(know["g"]), "rem" + s), parts, [])
        n = len(engines(src_core, core))
        final["a_" + name] = n
        last_w[name] = ("a_" + name, n, {}, "arr")
        late = REM + REM0 + 256 * cols / REM1
        calls.append(([("g", REM, late, issue)], parts, ["sent" + name]))
        calls.append(([("-", 0.0, 0.001, lambda: None)], ["sent" + name], [name]))

    def B(name, lo=0, hi=None, step=1, key=None, more=()):
        b, at, w, by = _WHERE[name]
        hi = w if hi is None else hi
        return (T[b][:, at + lo:at + hi:step] if step > 1 else T[b][:, at + lo:at + hi], key or name, tuple(more), (hi - lo + step - 1) // step, by)

    def P(i, lo, hi, step=1):
        t = T["p%d" % i]
        return (t[:, lo:hi:step] if step > 1 else t[:, lo:hi], "#%d" % i, (), (hi - lo + step - 1) // step, "psum")

    PARTS = {"xw": ("xwd",), "gw": ("gw0", "gw1", "gw2", "gw3", "gw4", "gw5"), "fw": ("fwa", "fwb"), "go": ("god",), "ball": ("balld",), "qr": ("qrd",),
             "cw": ("cwd",), "ra0": ("ra0d",), "ra1": ("ra1d",), "ra2": ("ra2d",), "lfo": ("lfd",), "yl0": ("yld", "yla", "ylb", "ylc")}

    def I(name, off):
        return (B(name)[0].indirect(off[0]), name, PARTS.get(name, ()) + (off[1],) + off[2], 16 * off[3], "list")

    def keys_in(ops):
        return [o[1] for o in ops] + [k for o in ops for k in o[2]]

    def time_v(out, ins, both=False):
        if out[4] == "list":
            return 0.05 + out[3] * SC * CY
        if ins and ins[0][4] == "list":
            return 0.05 + out[3] * GA * CY
        n = ins[0][3] if ins else out[3]
        if both:
            return max(64, n * (1 if "psum" in (ins[0][4], ins[1][4]) else 2)) * CY
        return max(64, n * (0.5 if all(o[4] == 2 for o in [out] + ins) else 1)) * CY

    def time_s(in_):
        return 0.065 + max(64, in_[3] * (GA if in_[4] == "list" else 1)) * CY

    def on_s(out, in_, func, bias=0.0, scale=1.0):
        x = bias[0] if isinstance(bias, tuple) else bias
        return ("s", time_s(in_), lambda e: e.activation(out=out[0], in_=in_[0], func=func, bias=x, scale=scale))

    def copy(out, in_, either=False):
        ways = [("v", time_v(out, [in_]), lambda e: e.tensor_copy(out=out[0], in_=in_[0]))]
        emit(keys_in([in_]) + list(out[2]), [out[1]], *(ways + [on_s(out, in_, AF.Copy)] * either))

    def tt(out, a, b, op):
        emit(keys_in([a, b]) + list(out[2]), [out[1]], ("v", time_v(out, [a, b], True), lambda e: e.tensor_tensor(out=out[0], in0=a[0], in1=b[0], op=op)))

    def ts(out, a, s1, op0, s2=None, op1=None, also=None):
        x1 = s1[0] if isinstance(s1, tuple) else s1
        x2 = s2[0] if isinstance(s2, tuple) else s2
        R = keys_in([x for x in (a, s1, s2) if isinstance(x, tuple)])
        if op1 is None:
            way = ("v", time_v(out, [a]), lambda e: e.tensor_scalar(out=out[0], in0=a[0], scalar1=x1, scalar2=None, op0=op0))
        else:
            way = ("v", time_v(out, [a]), lambda e: e.tensor_scalar(out=out[0], in0=a[0], scalar1=x1, scalar2=x2, op0=op0, op1=op1))
        emit(R, [out[1]], *([way] + ([on_s(out, a, *also)] if also else [])))

    def scan(out, d0, d1, init, op0, op1):
        x = init[0] if isinstance(init, tuple) else init
        emit(keys_in([o for o in (d0, d1, init) if isinstance(o, tuple)]), [out[1]],
             ("v", time_v(out, [d0, d1]), lambda e: e.tensor_tensor_scan(out=out[0], data0=d0[0], data1=d1[0], initial=x, op0=op0, op1=op1)))

    def total(out, in_):
        emit(keys_in([in_]), [out[1]], ("v", max(64, in_[3]) * CY, lambda e: e.tensor_reduce(out=out[0], in_=in_[0], axis=AxisListType.X, op=OP.add)))

    def fill(out, c):
        emit([], [out[1]], ("v", time_v(out, []), lambda e: e.memset(out[0], c)))

    def act(out, in_, func, bias=0.0, scale=1.0):
        emit(keys_in([in_]), [out[1]], on_s(out, in_, func, bias, scale))

    def signs(out, in_, bias, acc):
        emit(keys_in([in_, bias]), [out[1], acc[1]],
             ("s", time_s(in_) + 0.02, lambda e: e.activation(out=out[0], in_=in_[0], func=AF.Sign, bias=bias[0], scale=-1.0, accum_out=acc[0])))

    def mms(group):
        def step(o, a, b, start, stop):
            return lambda e: e.matmul(o[0], a[0], b[0], start, stop)
        R = sorted(set(keys_in([m[1] for m in group] + [m[2] for m in group])))
        emit(R, [group[0][0][1]], ("t", sum(max(min(64, m[1][3]), m[2][3]) for m in group) * PE, [step(*m) for m in group]))

    def mm(out, *pairs, start=True, stop=True):
        mms([(out, a, b, start and i == 0, stop and i == len(pairs) - 1) for i, (a, b) in enumerate(pairs)])

    def iota(out, pattern, base, cm):
        if out[4] == 2:
            emit([], [out[1]], ("g", 0.13 + 2 * out[3] * CY, lambda e: e.iota(out[0], pattern, base, cm, allow_small_or_imprecise_dtypes=True)))
        else:
            emit([], [out[1]], ("g", 0.13 + 2 * out[3] * CY, lambda e: e.iota(out[0], pattern, base, cm)))

    def select(out, in_, op):
        emit([in_[1]], [out[1]], ("g", 0.17 + 2 * out[3] * CY, lambda e: e.affine_select(out[0], in_[0], [[1, 128]], op, 0.0, 0, -1)))

    def wide(name, c):
        return B(name, 15 - c, 143 - c)

    def wrap(bk, lo, wname, rows, n, start=True, stop=True, first=0, key=None, more=()):
        mms([(P(bk, lo + first, lo + n), wide(wname, c), B(rows, 16 * first + c, 16 * n, 16, key=key, more=more), start and c == 0, stop and c == 15)
             for c in range(16)])

    def X(t, key, more=()):
        return (t, key, more)

    def col(f):
        return B("m16", f, f + 1)

    def to_row(f, name):
        dma("y", (T.t_gw[f:128:16, 0:W], "gw%d" % f, ("gw",)), B(name), 32)

    def disk_of(t):
        return cores[(rank + 1 + t) % N]

    def asker_of(t):
        return cores[(rank - 1 - t) % N]

    dma("y", B("cxi"), X(T.cx[:], "in"), 128)
    dma("s", B("qr", 0, K), X(T.qx[:], "in"), 64)
    dma("y", B("xw", 0, W), X(T.xr[:], "in"), 512)
    dma("s", B("tgi"), X(T.tg[:], "in"), 64)
    dma("y", B("lfo", 0, M), X(T.lf[:], "in", ("xw",)), 768)
    dma("y", B("xlo"), X(T.xl[:], "in", ("xw",)), 384)
    dma("y", B("fdi"), X(T.fd[:], "in", ("xw",)), 512)

    def constants():
        b16 = B("blk", 0, 128, 16)
        fill(B("ones"), 1.0)
        select(B("ib"), B("ones", 0, 128), OP.is_equal)
        iota(B("d1"), [[16, 8], [0, 16]], 15, -1)
        iota(B("pb"), [[0, 8], [-1, 16]], 0, 1)
        iota(B("ckey"), [[0, 8], [16, 16]], 0, 0)
        iota(B("ca"), [[1, 16]], 0, 0)
        iota(B("pc"), [[1, 1]], 0, 1)
        iota(B("kc"), [[0, 16], [1, 16]], 0, 0)
        iota(B("vhs"), [[16, 8], [0, 16]], 0, 128)
        iota(B("vlo"), [[0, 8], [1, 16]], 0, 0)
        for i in range(16):
            ts(B("rr", i, 2048, 16, key="rr%d" % i), B("ib"), -1.0, OP.mult, also=(AF.Copy, 0.0, -1.0))
        for name, lo, hi, key in (("gw", 0, WD, "gw"), ("xw", W, WD, "xwd"), ("yl0", M, MD, "yld"), ("ball", K, KD, "balld"), ("qr", K, KD, "qrd"),
                                  ("ra0", K, KD, "ra0d"), ("ra1", K, KD, "ra1d"), ("ra2", K, KD, "ra2d"), ("wb", 0, 144, "wb"), ("lp01", 0, 128, "lp01"),
                                  ("lp5", 0, 128, "lp5")):
            fill(B(name, lo, hi, key=key), 0.0)
        for name, lo, hi, key in (("fw", W, WD, "fw"), ("lfo", M, MD, "lfd"), ("cw", K, KD, "cwd"), ("ol", 0, 16, "ol")):
            fill(B(name, lo, hi, key=key), 0)
        copy(B("ih"), B("ib"))
        ts(B("d1s"), B("d1"), 4, OP.arith_shift_right)
        ts(B("pbs"), B("pb"), 15, OP.bitwise_and)
        ts(B("blk"), B("d1s"), 0.0, OP.is_equal)
        ts(B("maskb"), B("pbs"), 0.0, OP.is_equal)
        ts(B("m16"), B("pbs", 0, 16), 0.0, OP.is_equal)
        ts(B("sels"), b16, 32768.0, OP.mult)
        copy(B("blk16"), b16)
        copy(B("blkh"), B("blk"))
        copy(B("wb", 15, 143, 16), b16)
        copy(B("expl"), B("ca"))
        ts(B("zz2"), B("kc", 0, 128), 0.0, OP.is_equal, 2.0 * BIG, OP.mult)
        select(B("tri"), B("blk"), OP.is_gt)
        tt(B("imt"), B("ib"), B("tri"), OP.subtract)
        ts(B("bneg"), B("blk"), -2.0 ** 61, OP.mult, 2.0 ** 61, OP.mult)
        ts(B("re_"), B("bneg"), col(4), OP.mult, -1.0, OP.mult)
        ts(B("zz"), B("kc"), 0.0, OP.is_equal, 0.5, OP.mult)
        ts(B("z0"), B("zz"), 0.5, OP.add)
        ts(B("top"), B("ones", 0, 1), 2.0 ** 60, OP.mult, 2.0 ** 55, OP.mult)
        scan(B("thr"), B("z0"), B("ones"), B("top"), OP.mult, OP.mult)
        tt(B("z1"), B("thr", 0, 16), B("m16"), OP.mult)
        total(B("w15"), B("z1"))
        ts(B("pw"), B("w15"), 2.0 ** -50, OP.mult, 2.0 ** -50, OP.mult)
        ts(B("wdiag"), B("blk"), B("pw"), OP.mult)
        ts(B("pcs"), B("pc"), 15, OP.bitwise_and)
        copy(B("pm"), B("pcs"))
        ts(B("kw"), B("ca"), 16.0, OP.mult, B("pm"), OP.add)
        ts(B("kh5"), B("kw"), 0.5, OP.add)
        ts(B("dw"), B("kw", 0, 6), float(W), OP.add)
        ts(B("dw1"), B("kw", 0, 6), float(W + 1), OP.add)
        ts(B("dm"), B("kw", 0, 6), float(M + 5119), OP.add)
        tt(B("cn"), col(0), col(1), OP.add)
        tt(B("cv"), col(2), col(3), OP.add)
        tt(B("ck"), B("cn"), B("cv"), OP.add)
        tt(B("cy"), B("cv"), col(5), OP.add)
        ts(B("cz"), B("cn"), 2.0, OP.mult, col(4), OP.subtract)
        ts(B("cg"), col(2), FAR, OP.mult, col(4), OP.add)
        ts(B("ns"), col(0), -0.5, OP.mult, 1.0, OP.add)
        ts(B("nb"), col(0), 1279.75, OP.mult)
        ts(B("nw"), col(0), 4.0, OP.mult, col(1), OP.subtract)
        ts(B("go", K, KD, key="god"), B("ones", 0, 16), B("cg"), OP.mult)
        for name, c in (("wbn", B("cn")), ("wbv", B("cv")), ("wbh", col(0)), ("wbmh", B("nw")), ("wby", B("cz")), ("wb2", 2.0 ** -8), ("wb2n", -2.0 ** -8)):
            ts(B(name), B("wb"), c, OP.mult)
        for name, c, w in (("wbx", 5, 2.0 ** -9), ("wbxn", 5, -2.0 ** -9), ("wbf", 0, FAR)):
            ts(B(name), B("wb"), col(c), OP.mult, w, OP.mult)
        ts(B("rn"), B("blk"), B("cn"), OP.mult)
        ts(B("rp"), B("blk"), col(4), OP.mult)
        ts(B("lp1h"), B("blk"), 0.0, OP.mult)
        copy(B("lp01", 0, 128, 16), b16)
        ts(B("lp01", 1, 128, 16), b16, -1.0, OP.mult)
        copy(B("lp1h", 1, 128, 16), b16)
        copy(B("lp5", 5, 128, 16), b16)
        ts(B("ml"), B("ib"), B("ck"), OP.mult)
        for t in range(RO):
            tt(B("ld%d" % t), col(4), col(6 + t), OP.add)
            ts(B("mc%d" % t), B("ib"), B("cy"), OP.mult)
            ts(B("mc%d" % t, 4, 128, 16), b16, col(6 + t), OP.mult)

    def tables():
        ts(B("vht"), B("vhs"), 2047, OP.bitwise_and)
        copy(B("vhi"), B("vht"))
        ts(B("tl"), B("tgi"), 1, OP.arith_shift_right)
        ts(B("te"), B("tgi"), 1, OP.bitwise_and)
        copy(B("p0"), B("tl"))
        ts(B("pe"), B("te"), -1.0, OP.mult, 1.0, OP.add)
        tt(B("p1"), B("tl"), B("p0"), OP.subtract)
        mms([(P(6, 0, 128), wide("wb", c), B("xw", 128 * c, 128 * c + 128), c == 0, c == 15) for c in range(16)])
        copy(B("px"), P(6, 0, 128), True)
        for f, name in enumerate(("p0", "p1", "vhi", "vlo", "pe", "px")):
            to_row(f, name)
        copy(B("cu"), B("cxi"))
        for kh in range(2):
            mm(P(5, 128 * kh, 128 * kh + 128), (B("qr", 128 * kh, 128 * kh + 128), B("ib")))
        copy(B("qt"), P(5, 0, 256), True)

    def unpack():
        ts(B("fw", 0, 1024, key="fwa"), B("fdi"), 2047, OP.bitwise_and)
        ts(B("fw", 1024, 2048, key="fwb"), B("fdi"), 11, OP.arith_shift_right)

    def eqs(tile, rows, n, cols, bk, lo, among=None, start=False):
        width = 16 * n
        for j in range(n):
            e = B(tile, width * j + 16 * j, width * j + width, key="%s%d" % (tile, j))
            ts(e, B(rows[0], 16 * j, width, key=rows[1], more=rows[2:]), B(cols, j, j + 1), OP.is_equal, 2.0 ** (99 - 15 * j), OP.mult)
            mm(P(bk, lo + 16 * j, lo + width), (B("wdiag"), e), start=start and j == 0, stop=j == n - 1)
            if among and j in among:
                among[j]()

    RR = ["rr%d" % i for i in range(16)]

    def choice(t):
        copy(B("c16"), B("cu"))
        for kh in range(2):
            lo, hi, kb = 128 * kh, 128 * kh + 128, 3 + kh
            mm(P(kb, 0, 128), (B("c16", lo, hi), B("ih")), (B("ones", 0, 128), B("ckey")), stop=False)
            for j in range(4 * kh, 4 * kh + 4):
                xc, d = B("xc", 512 * j, 512 * j + 512, key="xc%d" % j), P(DB[j % len(DB)], 0, 512)
                copy(xc, I("xw", B("cu", 32 * j, 32 * j + 32)), True)
                mm(d, (B("ib"), xc), (B("qt", lo, hi), B("rr", 512 * (j % 4), 512 * (j % 4) + 512, key=RR[0], more=RR)))
                act(B("ab", 512 * j, 512 * j + 512, key="ab%d" % j), d, AF.Abs, bias=128.0 if t else 0.0)
            mms([(P(kb, i, 128, 16), B("ab", 2048 * kh + i, 2048 * kh + 2048, 16, key="ab%d" % (4 * kh), more=["ab%d" % j for j in range(4 * kh, 4 * kh + 4)]),
                  B("sels"), False, i == 15) for i in range(16)])
            e = B("expl", 8 * kh, 8 * kh + 8)
            scan(B("ks", lo, hi, key="ks%d" % kh), B("zz2"), P(kb, 0, 128), 0.0, OP.add, OP.min)
            ts(B("ol", 8 * kh, 8 * kh + 8), B("ks", lo + 15, hi, 16, key="ks%d" % kh), 2047, OP.bitwise_and)
            tt(B("olm", lo, hi, key="olm%d" % kh), I("ol", e), B("maskb"), OP.mult)
            mm(P(3, 256 + 8 * kh, 264 + 8 * kh), (B("olm", lo, hi, key="olm%d" % kh), B("blk16")))
            copy(B("ole", lo, hi, key="ole%d" % kh), I("ol", e))
            mm(P(kb, 128, 256), (B("ole", lo, hi, key="ole%d" % kh), B("ih")))
            copy(B("orh", lo, hi, key="orh%d" % kh), P(kb, 128, 256))
        copy(B("cw", 0, K), B("cu"))

    def requests(t):
        copy(B("olu"), P(3, 256, 272))
        copy(B("olf"), P(3, 256, 272))
        copy(B("go", 0, K), I("gw", B("olu")), True)
        wrap(0, 0, "wbn", "go", 16)
        copy(B("nlu"), P(0, 0, 16))
        send(disk_of(t), asker_of(t), "rq%d" % t, 16, "nlu", ["nlu"])
        eqs("eq", ("orh", "orh1", "orh0"), 16, "olf", 5, 0, {14: lambda: mm(P(5, 0, 256), (B("re_"), B("go", 0, K)), start=False, stop=False)}, start=True)
        tt(B("cand"), P(5, 0, 256), B("thr"), OP.is_lt)
        scan(B("cs"), B("ones"), B("cand"), 0.0, OP.mult, OP.add)
        a0, acc = 6 - ON_V, ["acc%d" % a for a in range(6)]
        for a in range(6):
            junk = B("junk", 256 * a, 256 * a + (256 if a < a0 else 256 - 16 * a0), key="junk%d" % a)
            if a < a0:
                signs(junk, B("cs"), B("kh5", a, a + 1), B("acc", a, a + 1, key=acc[a]))
            else:
                ts(junk, B("cs", 16 * a0, 256), B("kw", a, a + 1), OP.is_le)
                total(B("acc", a, a + 1, key=acc[a]), junk)
        ts(B("klu", a0, 6, key="klb"), B("acc", a0, 6, key=acc[5], more=acc[a0:]), 16.0 * a0, OP.add)
        ts(B("klu", 0, a0), B("acc", 0, a0, key=acc[0], more=acc[:a0]), 0.5, OP.mult, 128.0, OP.add)
        copy(B("sb"), I("lfo", B("rq%d" % t)))
        send(asker_of(t), disk_of(t), "rb%d" % t, K, "sb", ["sb"])
        copy(B("sa"), I("xlo", B("rq%d" % t)), True)
        send(asker_of(t), disk_of(t), "ra%d" % t, K, "sa", ["sa"])
        kl = B("klu", more=["klb"])
        copy(B("csu"), I("cw", kl))
        ts(B("qc"), I("qr", kl), -128.0 if t else 0.0, OP.add, also=(AF.Identity, -128.0 if t else 0.0))
        copy(B("sw"), I("go", kl), True)
        wrap(1, 0, "wbv", "sw", 6)
        tt(B("u1"), P(1, 0, 6), B("dw"), OP.min)
        copy(B("osu"), B("u1"))
        for i in range(16):
            copy(B("qe", i, 1536, 16, key="qe%d" % i), B("qc"), True)
        copy(B("ball", 0, K), B("rb%d" % t))
        act(B("s1"), I("ball", kl), AF.Square, bias=8.0, scale=2.0)
        act(B("s2"), I("ball", kl), AF.Square, bias=592.0)
        copy(B("bf"), I("ball", kl), True)
        copy(B("at"), I("ra%d" % t, kl), True)
        for c, (s, add) in enumerate((("s1", 32.0 * 2046), ("s2", 32.0 * 1337))):
            lo, hi = 96 * c, 96 * c + 96
            ts(B("ci", lo, hi, key="ci%d" % c), B(s), add, OP.add)
            ts(B("cm", lo, hi, key="cm%d" % c), B("ci", lo, hi, key="ci%d" % c), 5, OP.arith_shift_right, 2047, OP.bitwise_and)
            copy(B("cl12", lo, hi, key="cl%d" % c), B("cm", lo, hi, key="cm%d" % c))

    def disk_writes(t):
        for h in range(3):
            copy(B("gs", 512 * h, 512 * h + 512, key="gs%d" % h), I("gw", B("csu", 32 * h, 32 * h + 32)), True)
        wrap(6, 0, "wbn", "gs", 96, key="gs0", more=("gs1", "gs2"))
        copy(B("db", 6, DW, key="dbb"), P(6, 0, 96))
        mm(P(7, 0, 96), (B("rn"), B("sw")))
        wrap(7, 96, "wbn", "sw", 6)
        copy(B("nrh"), P(7, 0, 96))
        copy(B("nl"), P(7, 96, 102), True)
        mm(P(7, 128, 224), (B("re_"), B("sw")), stop=False)
        ts(B("nh"), B("nrh"), B("ns"), OP.mult, B("nb"), OP.add)
        wrap(0, 128, "wbmh", "nh", 6, stop=False)
        eqs("eqn", ("nrh", "nrh"), 6, "nl", 7, 128)
        tt(B("lsn"), P(7, 128, 224), B("thr", 0, 96), OP.is_ge)
        wrap(0, 128, "wbf", "lsn", 6, start=False)
        tt(B("u2"), P(0, 128, 134), B("dm"), OP.min)
        ts(B("db", 0, 6, key="dba"), B("u2"), -5119.0, OP.add)
        send(disk_of(t), asker_of(t), "rd%d" % t, DW, "db", ["dba", "dbb"])

    def apply(dst, t):
        copy(I(dst, B("rd%d" % t, 0, 6)), B("rd%d" % t, 6, DW))

    QE = ["qe%d" % i for i in range(16)]

    def translate(t):
        def piece(c, lo, hi, key):
            cl = B("cl12", 96 * c + lo, 96 * c + hi, key="cl%d" % c)
            tt(B("m%d" % (c + 1), 16 * lo, 16 * hi, key="m" + key), I("xw", cl), B("qe", 16 * lo, 16 * hi, key="qe0", more=QE), OP.max)
            copy(B("g%d" % (c + 1), 16 * lo, 16 * hi, key="g" + key), I("gw", cl), True)
        piece(0, 0, 48, "1a")
        piece(0, 48, 96, "1b")
        piece(1, 0, HALF, "2a")
        piece(1, HALF, 96, "2b")
        wrap(4, 0, "wbn", "g1", 96, key="g1a", more=("g1b",))
        tt(B("e1"), P(4, 0, 96), B("bf"), OP.is_equal)
        wrap(3, 0, "wbx", "g1", 96, stop=False, key="g1a", more=("g1b",))
        wrap(3, 0, "wb2n", "m1", 96, start=False, stop=False, key="m1a", more=("m1b",))
        wrap(5, 0, "wbn", "g2", HALF, key="g2a")
        wrap(3, 0, "wbxn", "g2", HALF, start=False, stop=False, key="g2a")
        wrap(3, 0, "wb2", "m2", HALF, start=False, stop=False, key="m2a")
        wrap(5, 0, "wbn", "g2", 96, first=HALF, key="g2b")
        wrap(3, 0, "wbxn", "g2", 96, start=False, stop=False, first=HALF, key="g2b")
        wrap(3, 0, "wb2", "m2", 96, start=False, first=HALF, key="m2b")
        copy(I("xw", B("osu")), B("at"))
        copy(B("xo"), I("xw", B("olu")), True)
        tt(B("dcf"), B("cm", 96, 192, key="cm1"), B("cm", 0, 96, key="cm0"), OP.subtract)
        tt(B("e2"), P(5, 0, 96), B("bf"), OP.is_equal)
        tt(B("wf"), P(3, 0, 96), B("e2"), OP.max)
        tt(P(4, 128, 224), B("wf"), B("e1"), OP.is_gt)
        tt(P(4, 256, 352), P(4, 128, 224), B("dcf"), OP.mult)
        tt(B("sf"), P(4, 256, 352), B("cm", 0, 96, key="cm0"), OP.add)
        copy(I("fw", B("osu")), B("sf"))

    def moves(t):
        last = t == RO - 1
        copy(B("ycf") if last else B("cu"), I("fw", B("olu")))
        bias = 63.75 if t else 127.75
        if not last:
            for kh in range(2):
                lo, hi = 128 * kh, 128 * kh + 128
                mm(P(2, lo, hi), (B("xo", lo, hi), B("ib")), (B("qr", lo, hi), B("ib")))
            ts(B("qt"), P(2, 0, 256), 0.5, OP.mult, bias, OP.add, also=(AF.Identity, bias, 0.5))
        mm(P(1, 256, 512), (B("ib"), B("xo")), (B("ib"), B("qr", 0, K)))
        ts(B("qr", 0, K), P(1, 256, 512), 0.5, OP.mult, bias, OP.add, also=(AF.Identity, bias, 0.5))
        if last:
            ts(B("yqb"), B("qr", 0, K), -128.0, OP.add, also=(AF.Identity, -128.0))

    def claims(t):
        mm(P(6, 256, 352), (B("ml"), B("sw")), (B("lp5"), B("at")))
        ts(B("gl"), P(6, 256, 352), B("ld%d" % t), OP.add, also=(AF.Identity, B("ld%d" % t)))
        copy(I("gw", B("osu")), B("gl"))
        mm(P(5, 128, 224), (B("rp"), B("sw")), (B("ib"), B("e1")), (B("ib"), B("e2")))
        ts(B("nr"), P(5, 128, 224), 0.0, OP.is_equal, also=(AF.Relu, 1.0, -1.0))
        mm(P(5, 256, 352), (B("imt"), B("nr")))
        ts(B("f1"), P(5, 256, 352), 0.0, OP.max, also=(AF.Relu,))
        tt(B("fv"), B("f1"), B("sf"), OP.mult)
        mm(P(5, 384, 480), (B("blkh"), B("fv")), (B("blk"), B("f1")))
        tt(B("fb"), B("f1"), B("bf"), OP.mult)
        copy(B("fb0"), B("fb"))
        copy(B("vrh"), P(5, 384, 480))
        wrap(5, 0, "wbh", "vrh", 6)
        mm(P(7, 384, 480), (B("re_"), B("ones", 0, 96)), (B("bneg"), B("f1")), stop=False)
        copy(B("vl"), P(5, 0, 6), True)
        eqs("eqc", ("vrh", "vrh"), 6, "vl", 7, 384)
        tt(B("lsc"), P(7, 384, 480), B("thr", 0, 96), OP.is_ge)
        wrap(5, 16, "wbf", "lsc", 6)
        tt(B("u4"), P(5, 16, 22), B("vl"), OP.max)
        tt(B("u3"), B("u4"), B("dw1"), OP.min)
        ts(B("vu"), B("u3"), -1.0, OP.add)
        copy(B("old"), I("gw", B("vu")), True)
        mm(P(7, 0, 96), (B("lp01"), B("fb0")), (B("lp1h"), B("fb")), (B("mc%d" % t), B("old")))
        copy(B("gn"), P(7, 0, 96), True)
        copy(I("gw", B("vu")), B("gn"))

    constants()
    tables()
    for t in range(RO):
        choice(t)
        requests(t)
        if t == 0:
            unpack()
        if t == RO - 1:
            for h in range(3):
                copy(B("yl0", 512 * h, 512 * h + 512, key="yl" + "abc"[h]), B("lfo", 512 * h, 512 * h + 512))
        disk_writes(t)
        translate(t)
        moves(t)
        claims(t)
        apply("lfo" if t < RO - 1 else "yl0", t)
    dma("y", X(T.yl[:], "yl"), B("yl0", 0, M, more=PARTS["yl0"]), 768)
    dma("y", X(T.yc[:], "yc"), B("ycf"), 128)
    dma("y", X(T.yq[:], "yq"), B("yqb"), 64)
    mms([(P(0, 0, 128), wide("wby", c), B("gw", 128 * c, 128 * c + 128), c == 0, c == 15) for c in range(16)])
    ts(B("ytf"), P(0, 0, 128), 1.0, OP.add, also=(AF.Identity, 1.0))
    dma("y", X(T.yt[:], "yt"), B("ytf"), 64)
    if not ORDER:
        ORDER.extend(in_order(calls))
    for n, way in ORDER:
        calls[n][0][way][3]()
    for s in sorted(final):
        if know["g"].get(s, 0) < final[s]:
            g.wait_ge(T.sem[s], final[s])
